import numpy as np, ml_dtypes
CORES = [16,18,20,22]
N = 4
import mx_ref
BF = ml_dtypes.bfloat16
def gentries(a):
    return np.ascontiguousarray(a.reshape(8, 16, -1).transpose(0, 2, 1)).reshape(8, -1)
def gtable(e):
    e = np.asarray(e); return np.ascontiguousarray(e.reshape(8, -1, 16).transpose(0, 2, 1)).reshape(128, -1).astype(np.int32)
def gcols(t, e):
    v = np.concatenate([t.reshape(8, 16, -1, 4), np.zeros((8, 16, 1, 4), BF)], axis=2)
    return np.ascontiguousarray(np.stack([v[g][:, e[g]] for g in range(8)])).reshape(128, -1)
def tile(rs):
    return np.stack(rs, axis=2).reshape(128, -1).astype(BF)
def pick(q, e):
    c = np.concatenate([q[0].reshape(128, -1, 4), np.zeros((128, 1, 4), np.uint8)], axis=1); s = np.concatenate([q[1], np.ones((16, 1), np.uint8)], axis=1)
    return (np.ascontiguousarray(c[:, e].reshape(128, -1)), np.ascontiguousarray(s[:, e]))
def join(*qs):
    return (np.concatenate([q[0] for q in qs], axis=1), np.concatenate([q[1] for q in qs], axis=1))
def put(q, e, v):
    c, s = q[0].reshape(128, -1, 4).copy(), q[1].copy(); c[:, e] = v[0].reshape(128, -1, 4); s[:, e] = v[1]
    return (c.reshape(128, -1), s)
def pk(c, s):
    return (np.ascontiguousarray(c), mx_ref.live(s))
def emit(q):
    return q[0], q[1]
def packed(v, rng):
    q = [mx_ref.quantize(np.ascontiguousarray(v[r])) for r in range(N)]
    return np.stack([a for a, b in q]), np.stack([mx_ref.plane(b, rng) for a, b in q])
def values_of_codes():
    e, c = np.zeros((128, 128, 4), np.float32), np.zeros((128, 2, 4), np.uint8)
    e[np.arange(128), np.arange(128), 0] = 1
    c[:127, :, 0] = np.arange(256).reshape(2, 128).T[:127]
    return mx_ref.matmul(mx_ref.quantize(e.reshape(128, 512).astype(BF)), (c.reshape(128, 8), np.full((16, 2), 127, np.uint8))).T.reshape(-1).astype(np.float64)
CODE_VALUE, SCALE_VALUE = values_of_codes(), 2.0 ** (np.arange(256) - 127.0)
def decode(q):
    return (CODE_VALUE[q[0]].reshape(16, 8, -1, 4) * SCALE_VALUE[q[1]][:, None, :, None] + 0.0).reshape(128, -1).astype(np.float32)
def f(rng, *shape):
    return mx_ref.flush((rng.standard_normal(shape, dtype=np.float32) * np.exp2(rng.integers(-2, 3, shape[:-1] + (1,)))).astype(BF))
def wide(rng, *shape, cols=0):
    v = rng.standard_normal(shape, dtype=np.float32) * np.exp2(rng.integers(-12, 13, shape)).astype(np.float32)
    if cols: v *= np.repeat(np.exp2(rng.integers(-cols, cols + 1, shape[:-2] + (1, shape[-1] // 4))) * (rng.random(shape[:-2] + (1, shape[-1] // 4)) > 0.0625), 4, axis=-1).astype(np.float32)
    return mx_ref.flush(v.astype(BF))
C = 384
STEP = [1, 2, 3]
def numbers_of(rng):
    return {"x": np.array(f(rng, N, 128, 4 * C)), "u": np.array(f(rng, N, 128, 512)), "v": np.array(f(rng, N, 128, 512))}
def stored(w):
    return {"wl": np.stack([gtable(w[r]) for r in range(N)])}
def joined(k):
    w = np.zeros_like(k)
    np.put_along_axis(w, k[..., 0::2], k[..., 1::2], axis=-1)
    np.put_along_axis(w, k[..., 1::2], k[..., 0::2], axis=-1)
    return w
def wiring(rng):
    return stored(joined(rng.permuted(np.tile(np.arange(3 * C), (N, 8, 1)), axis=2)))
def edges(rng):
    w = np.zeros((N, 8, 3 * C), np.int64)
    c, i = np.arange(C), np.arange(3 * C)
    for r in range(N):
        a = C + rng.permutation(2 * C)
        k = [i ^ 1, 3 * C - 1 - i, (i + 3 * (C // 2)) % (3 * C), np.concatenate([c + C, c, (c ^ 1) + 2 * C]), np.concatenate([C - 1 - c, c + 2 * C, c + C]),
             joined(np.concatenate([rng.permutation(C), C + rng.permutation(2 * C)])), joined(np.concatenate([np.stack([c, a[:C]], axis=1).reshape(-1), a[C:]])), joined(rng.permutation(3 * C))]
        w[r, rng.permutation(8)] = np.stack(k)
    return stored(w)
def layers(rng):
    return np.array(f(rng, N, 128, 2048)).reshape(N, 8, 16, 4, 8, 16, 4)
def weights(rng, w):
    c, p = packed(np.ascontiguousarray(w).reshape(N, 128, 2048), rng)
    return {"wc": c, "ws": p}
def blank(d):
    u = d["u"].reshape(N, 128, 128, 4)
    u[:, :, 0::16] = 0
    u[:, :, 1::16] = 0
    return u
def setup_inputs(rng):
    return {**numbers_of(rng), **wiring(rng), **weights(rng, layers(rng))}
def setup_inputs_ties(rng):
    d = numbers_of(rng)
    o = rng.permutation(N)
    k = rng.integers(-1, 2, (N, 8, 2, C)).astype(np.float32)
    k[o[1]] = 1
    x = d["x"].reshape(N, 8, 16, C, 4)
    x[:, :, :3] = 0
    x[:, :, :2, :, 0] = k.astype(BF)
    x[:, :, 2, :, 0] = 1.96875 * 2.0 ** 7
    x[:, :, 3] = (np.array([9.0, 11.0, 5.0, 7.0]) * 2.0 ** -9).astype(np.float32).astype(BF)
    a = np.exp2(rng.integers(-3, 4, (1, 8, 1)).astype(np.float32))
    x[:, :, 8:] = 0
    x[:, :, 8, :, 0] = (-1.125 * a).astype(BF)
    x[:, :, 10, :, 0] = (-0.0703125 * a).astype(BF)
    c = np.ones(N, np.float32)
    c[o[0]] = 0
    c[o[2]] = -1
    u = blank(d)
    for h in range(0, 128, 16):
        for i in range(2): u[:, h + i, h + i, 0] = c.astype(BF)
    w = layers(rng)
    w[:, :, 2] = 0
    w[:, :, :, :, :, :4] = 0
    w[:, :, :, :, :, 8:] = 0
    for g in range(8):
        w[:, g, 8, 0, g, 8, 0] = -28.0
        for b in range(4):
            w[:, g, 10, b, g, 9, 0] = -2.0 ** (b - 5)
            w[:, g, 3, b, g, 3, b] = 64.0
    return {"x": x.reshape(N, 128, 4 * C), "u": u.reshape(N, 128, 512), "v": d["v"], **wiring(rng), **weights(rng, w)}
def setup_inputs_near(rng):
    d = numbers_of(rng)
    o = np.zeros(N, np.int64)
    for i, r in enumerate(rng.permutation([r for r in range(N) if r < (r ^ STEP[0])])):
        o[[r, r ^ STEP[0]]] = rng.permutation([0, 3] if i % 2 == 0 else [1, 2])
    x = d["x"].astype(np.float32).reshape(N, 8, 16, C, 4)
    x[:, :, :8] = 0
    u = blank(d)
    at = [0, C - 1, int(rng.integers(C)), int(rng.integers(C))]
    for r in range(N):
        s = rng.integers(-1, 2, (2, 8, C)).astype(np.float32)
        k = 2.0 ** -30 if o[r] in (0, 3) else 1.0
        for i in range(2):
            if o[r] == 2: x[r, :, 2 * i, :, 0] = s[i] * 2.0 ** -8
            else:
                x[r, :, 2 * i, :, 0] = 1.125 * k * s[i]
                x[r, :, 2 * i + 1, :, 0] = -1.25 * k * s[i]
                for g, j in zip(rng.permutation(8)[:4], at): x[r, g, 2 * i, j, 0] = 2.0 ** 30 * rng.choice([-1.0, 1.0])
            for h in range(0, 128, 16):
                u[r, h + 2 * i, h + i, 0] = 1.125 * k
                u[r, h + 2 * i + 1, h + i, 0] = k
        if o[r] == 2: x[r, :, 4, :, 0] = 1.96875 * 2.0 ** 8
        x[r, :, 5, :, 0] = rng.choice([-1.0, 1.0], (8, C)) * 2.0 ** -30
        x[r, :, 6, :, 0] = 2.0 ** -28
    w = layers(rng)
    w[:, :, :8] = 0
    w[:, :, :, :, :, :8] = 0
    for g in range(8):
        w[:, g, 5, 0, g, 0, 0] = 2.0 ** -8
        w[:, g, 5, 0, g, 2, 0] = 2.0 ** -8
        w[:, g, 5, 0, g, 6, 0] = 32.0
    return {"x": x.reshape(N, 128, 4 * C).astype(BF), "u": u.reshape(N, 128, 512), "v": d["v"], **wiring(rng), **weights(rng, w)}
def setup_inputs_late(rng):
    d = numbers_of(rng)
    c = (rng.permutation(N) % 2 * 2.0 - 1.0).astype(np.float32).astype(BF)
    x = d["x"].reshape(N, 8, 16, C, 4)
    x[:, :, :2] = c[:, None, None, None, None]
    u = blank(d)
    for h in range(0, 128, 16):
        for i in range(2): u[:, h + i, h + i, 0] = 1
    w = layers(rng)
    w[:, :, :, :, :, :2] = (w[:, :, :, :, :, :2].astype(np.float32) * 4).astype(BF)
    return {"x": x.reshape(N, 128, 4 * C), "u": u.reshape(N, 128, 512), "v": d["v"], **edges(rng), **weights(rng, w)}
def setup_inputs_ends(rng):
    d = numbers_of(rng)
    e = [0, STEP[0], STEP[1], STEP[0] ^ STEP[1]]
    e = e + [STEP[2] ^ i for i in e[:N - 4]]
    n = N // 4
    o = np.zeros(N, np.int64)
    o[np.array(e) ^ int(rng.integers(N))] = np.concatenate([np.full(n, 3), np.full(n, 2), rng.permutation(np.arange(2 * n) % 2)])
    x = np.zeros((N, 128, C, 4))
    u = blank(d).astype(np.float32)
    v = rng.choice([-1.0, 1.0], (N, 128, 512))
    w = np.zeros((N, 128, 4, 128, 4), np.float32)
    p = np.arange(128)
    for r in range(N):
        x[r] = (0.9 + 0.02 * rng.random((128, C, 4))) * 2.0 ** 30
        if o[r] == 0: x[r] *= -1
        if o[r] == 1: x[r] *= (1.0 - 2.0 * (np.arange(C) % 2))[None, :, None]
        if o[r] == 2: x[r] *= rng.choice([-1.0, 1.0], (128, C, 4))
        if o[r] == 3:
            x[r] = (1.0 + 0.125 * rng.integers(0, 8, (128, C, 4))) * 2.0 ** -30 * rng.choice([-1.0, 1.0], (1, C, 1))
            x[r, 0::8, :, 0] = 1.5 * 2.0 ** -29
        for i in range(2):
            h = rng.permutation(8)
            u[r, :, i::16] = np.where(h < 2, 0.0, h % 2 * 2.0 - 1.0)[None, :, None] * (2.0 ** -30 if o[r] == 3 else 2.0 ** 30)
        v[r] *= 2.0 ** 30 if o[r] % 2 == 0 else 2.0 ** -30
        for b in range(4): w[r, p, b, p, b] = [-0.25, -0.25, 2.0 ** -8, 256.0][o[r]]
    return {"x": x.astype(np.float32).reshape(N, 128, 4 * C).astype(BF), "u": u.reshape(N, 128, 512).astype(BF), "v": v.astype(np.float32).astype(BF), **edges(rng), **weights(rng, w.astype(BF))}
def setup_inputs_spread(rng):
    d = setup_inputs(rng)
    d["x"] = wide(rng, N, 128, 4 * C, cols=6)
    return d
def check_inputs(d):
    b = []
    for k in ("x", "u", "v"):
        a = np.abs(d[k].astype(np.float32))
        if not (np.isfinite(a).all() and ((a == 0) | (a >= 2.0 ** -30) & (a <= 2.0 ** 30)).all()): b.append("a value of " + k)
    none, least, most = [emit(mx_ref.quantize(np.full((128, 16), k, np.float32).astype(BF)))[1][0, 0] for k in (0.0, 2.0 ** -8, 2.0 ** 8)]
    for r in range(N):
        e, i = gentries(d["wl"][r]), np.arange(3 * C)
        if not ((e >= 0) & (e < 3 * C)).all(): b.append("an entry of wl")
        elif (e == i).any() or (np.take_along_axis(e, e, axis=1) != i).any(): b.append("wl: ports that aren't wired in pairs")
        if ((d["wc"][r] == 0x7F) | (d["wc"][r] == 0xFF)).any(): b.append("wc: a code that is no number")
        s = mx_ref.live(d["ws"][r])
        if ((s != none) & ((s < least) | (s > most))).any(): b.append("ws: a scale out of range")
    return b
def rewired(w, a, b):
    c, d = np.arange(C), w[:, :C]
    active = d < C
    same = a == np.take_along_axis(a, np.minimum(d, C - 1), axis=1)
    turn, cross, swap = active & same, active & ~same, ~active & b
    to = np.concatenate([np.where(turn | swap, c + C, c),
                         np.where(turn, c + 2 * C, np.where(cross, d + C, np.where(swap, c, c + C))),
                         np.where(turn, c, np.where(cross, d + 2 * C, c + 2 * C))], axis=1)
    new = np.zeros_like(to)
    np.put_along_axis(new, to, np.take_along_axis(to, w, axis=1), axis=1)
    return new
def reference(x, u, v, wl, wc, ws):
    qu = [mx_ref.quantize(u[r]) for r in range(N)]
    lay = [pk(wc[r], ws[r]) for r in range(N)]
    wire = [gentries(wl[r]).astype(np.int64) for r in range(N)]
    now = [x[r] for r in range(N)]
    for step in STEP:
        made = []
        for r in range(N):
            s = mx_ref.matmul(qu[r], mx_ref.quantize(now[r]))
            wire[r] = rewired(wire[r], s[0::16] > 0, s[1::16] > 0)
            one, two = gcols(now[r], wire[r][:, C:2 * C] % C), gcols(now[r], wire[r][:, 2 * C:] % C)
            z = mx_ref.quantize(((one.astype(np.float32) + two.astype(np.float32)) * np.float32(0.5)).astype(BF))
            made.append(mx_ref.quantize(tile([mx_ref.matmul(pick(lay[r], np.arange(128 * b, 128 * b + 128)), z) * np.float32(0.03125) for b in range(4)])))
        for r in range(N):
            p = r ^ step
            m = np.take_along_axis(wire[p], wire[r][:, :C], axis=1) % C
            now[r] = (now[r].astype(np.float32) + gcols(decode(made[p]).astype(BF), m).astype(np.float32)).astype(BF)
    y, ow = np.zeros((N, 128, C), np.float32), np.zeros((N, 8, 3 * C), np.float32)
    oc, osc = np.zeros((N, 128, 4 * C), np.uint8), np.zeros((N, 16, C), np.uint8)
    for r in range(N):
        q = mx_ref.quantize(now[r])
        y[r] = mx_ref.matmul(mx_ref.quantize(v[r]), q)
        ow[r] = wire[r]
        oc[r], osc[r] = emit(q)
    return {"y": y, "ow": ow, "oc": oc, "osc": osc}

@@ -1,0 +1,424 @@
+from concourse.mybir import dt, AluOpType, ActivationFunctionType as AF
+
+OP = AluOpType
+C = 384
+F = 3 * C
+K = 4194304.0
+ROUNDS = 3
+STEP = [1, 2, 3]
+RUNS = [(0, 192), (192, 384)]
+EXCHANGE = [RUNS, RUNS, [(0, 128), (128, 256), (256, 384)]]
+ZRUNS = [(0, 256), (256, 384)]
+
+SCRATCH = {
+    "xt": ("sbuf", [128, 4 * C], "bfloat16"), "xh": ("sbuf", [128, 4 * C], "bfloat16"), "gz": ("sbuf", [128, 4 * C], "bfloat16"),
+    "zt": ("sbuf", [128, 4 * C], "bfloat16"), "hp": ("sbuf", [128, 4 * C], "bfloat16"), "hg": ("sbuf", [128, 4 * C], "bfloat16"),
+    "ut": ("sbuf", [128, 512], "bfloat16"), "vt": ("sbuf", [128, 512], "bfloat16"),
+    "ones": ("sbuf", [128, F], "bfloat16"), "eb": ("sbuf", [128, 516], "bfloat16"),
+    "uq": ("sbuf", [128, 128], "float8_e4m3fn_x4"), "us": ("sbuf", [128, 128], "uint8"),
+    "pq": ("sbuf", [128, 256], "float8_e4m3fn_x4"), "psc": ("sbuf", [128, 256], "uint8"),
+    "vq": ("sbuf", [128, 128], "float8_e4m3fn_x4"), "vs": ("sbuf", [128, 128], "uint8"),
+    "em": ("sbuf", [128, 256], "float8_e4m3fn_x4"), "ems": ("sbuf", [128, 256], "uint8"), "el": ("sbuf", [128, 256], "float8_e4m3fn_x4"), "els": ("sbuf", [128, 256], "uint8"),
+    "sg": ("sbuf", [128, 192], "float32"),
+    "wq": ("sbuf", [128, 512], "float8_e4m3fn_x4"), "wp": ("sbuf", [128, 512], "uint8"),
+    "xq": ("sbuf", [128, C], "float8_e4m3fn_x4"), "xs": ("sbuf", [128, C], "uint8"),
+    "zq": ("sbuf", [128, C], "float8_e4m3fn_x4"), "zs": ("sbuf", [128, C], "uint8"),
+    "wlt": ("sbuf", [128, 72], "int32"), "pi32": ("sbuf", [128, 1], "int32"), "p15i": ("sbuf", [128, 1], "int32"),
+    "p15": ("sbuf", [128, 1], "float32"), "p3": ("sbuf", [128, 1], "float32"), "last": ("sbuf", [128, 1], "float32"),
+    "inv": ("sbuf", [128, 1], "float32"), "inv3": ("sbuf", [128, 1], "float32"), "thp": ("sbuf", [128, 1], "float32"),
+    "c48": ("sbuf", [128, 24], "float32"), "c3": ("sbuf", [128, 24], "float32"),
+    "uoi": ("sbuf", [128, 16], "int32"), "uo": ("sbuf", [128, 16], "uint16"),
+    "np15": ("sbuf", [128, 1], "float32"), "np16": ("sbuf", [128, 1], "float32"),
+    "jr": ("sbuf", [128, 96], "float32"), "e0": ("sbuf", [128, 96], "float32"), "e1": ("sbuf", [128, 96], "float32"), "e2": ("sbuf", [128, 96], "float32"), "e3": ("sbuf", [128, 96], "float32"), "mask": ("sbuf", [128, C], "float32"),
+    "idr": ("sbuf", [128, F], "float32"), "qtab": ("sbuf", [128, F], "float32"), "acttab": ("sbuf", [128, F], "bfloat16"),
+    "pir": ("sbuf", [128, F], "float32"), "om0": ("sbuf", [128, F], "float32"), "om1": ("sbuf", [128, F], "float32"),
+    "ew": ("sbuf", [128, 2 * C], "float32"), "hrow": ("sbuf", [128, C], "float32"), "thr": ("sbuf", [128, C], "float32"),
+    "fr": ("sbuf", [128, C], "float32"), "fs": ("sbuf", [128, C], "float32"),
+    "sc": ("sbuf", [128, F], "float32"), "y12": ("sbuf", [128, 2 * C], "float32"), "sy": ("sbuf", [128, 2 * C], "float32"),
+    "mr": ("sbuf", [128, C], "float32"), "ms": ("sbuf", [128, C], "float32"), "ml": ("sbuf", [128, 24], "uint16"),
+    "l12": ("sbuf", [128, 48], "uint16"),
+    "q3": ("sbuf", [128, 72], "float32"), "k1": ("sbuf", [128, 72], "float32"), "k2": ("sbuf", [128, 72], "float32"), "kk": ("sbuf", [128, 72], "float32"),
+    "u0": ("sbuf", [128, 72], "float32"), "du": ("sbuf", [128, 72], "float32"), "w12": ("sbuf", [128, 48], "float32"),
+    "p0": ("sbuf", [128, 72], "float32"), "dp": ("sbuf", [128, 72], "float32"),
+    "mp": ("sbuf", [128, 72], "float32"), "sp": ("sbuf", [128, 72], "float32"), "p16": ("sbuf", [128, 72], "uint16"),
+    "mu": ("sbuf", [128, 72], "float32"), "su": ("sbuf", [128, 72], "float32"), "u16": ("sbuf", [128, 72], "uint16"),
+    "ai": ("sbuf", [128, 24], "int32"), "a3": ("sbuf", [128, 24], "float32"), "act": ("sbuf", [128, 24], "float32"),
+    "td": ("sbuf", [128, 24], "float32"), "ta": ("sbuf", [128, 24], "float32"), "tau": ("sbuf", [128, 24], "float32"),
+    "ad0": ("sbuf", [128, 24], "float32"), "ad": ("sbuf", [128, 24], "float32"), "x12": ("sbuf", [128, 48], "uint16"),
+    "a2m": ("sbuf", [128, 24], "float32"), "va": ("sbuf", [128, 24], "float32"), "vta": ("sbuf", [128, 24], "float32"), "ss": ("sbuf", [128, 24], "float32"),
+    "u10": ("sbuf", [128, 24], "float32"), "u12": ("sbuf", [128, 24], "float32"), "dst": ("sbuf", [128, 24], "uint16"),
+    "w16": ("sbuf", [128, 72], "uint16"), "fin": ("sbuf", [128, 72], "uint16"), "owr": ("sbuf", [128, F], "float32"), "yt": ("sbuf", [128, C], "float32"),
+    "ps": ("psum", [128, 4096], "float32"),
+}
+for _k in range(ROUNDS):
+    SCRATCH["dl%d" % _k] = ("sbuf", [128, 24], "uint16")
+    SCRATCH["la%d" % _k] = ("sbuf", [128, 24], "uint16")
+    for _n in ("h", "l"):
+        SCRATCH["%sq%d" % (_n, _k)] = ("sbuf", [128, C], "float8_e4m3fn_x4")
+        SCRATCH["%ss%d" % (_n, _k)] = ("sbuf", [128, C], "uint8")
+SEMAPHORES = ["V", "A", "P", "G", "left", "ae"] + ["al%d" % k for k in range(ROUNDS)] + ["ah%d%d" % (k, i) for k in range(ROUNDS) for i in range(len(EXCHANGE[k]))] + ["d%d" % i for i in range(40)]
+
+
+def rank_program(g, core, T, topo):
+    rank = T.rank_of(core)
+    if rank is None:
+        return
+    QUEUE = {"V": g.vector, "A": g.scalar, "P": g.tensor, "G": g, "S": g.sync}
+    count = {}
+    seen = {}
+    book = {}
+
+    def wait(q, sem, val):
+        if seen.get((q, sem), 0) < val:
+            QUEUE[q].wait_ge(T.sem[sem], val)
+            seen[(q, sem)] = val
+
+    def region(r):
+        if len(r) == 3: return r[0], r[1], r[2], 1, 0
+        return r[0], r[1], r[2], r[3], r[1] % r[3]
+
+    def meets(a, b):
+        if a[0] >= b[1] or b[0] >= a[1]: return False
+        return not (a[2] == b[2] and a[3] != b[3])
+
+    def note(sem, val, reads, writes):
+        for r in reads:
+            n, lo, hi, st, ph = region(r)
+            book.setdefault(n, []).append((lo, hi, st, ph, sem, val, False))
+        for r in writes:
+            n, lo, hi, st, ph = region(r)
+            l = [e for e in book.get(n, []) if not (lo <= e[0] and e[1] <= hi and (st == 1 or (st, ph) == (e[2], e[3])))]
+            book[n] = l + [(lo, hi, st, ph, sem, val, True)]
+
+    def depend(q, reads, writes):
+        need = {}
+        for rs, w in ((reads, False), (writes, True)):
+            for r in rs:
+                n, lo, hi, st, ph = region(r)
+                for e in book.get(n, []):
+                    if (w or e[6]) and meets((lo, hi, st, ph), e): need[e[4]] = max(need.get(e[4], 0), e[5])
+        for sem in sorted(need): wait(q, sem, need[sem])
+
+    def op(q, reads, writes, call):
+        depend(q, reads, writes)
+        count[q] = count.get(q, 0) + 1
+        call(QUEUE[q]).then_inc(T.sem[q], 1)
+        note(q, count[q], reads, writes)
+
+    ndma = [0]
+
+    def dma(q, out, in_, reads, writes):
+        depend(q, reads, writes)
+        sem = "d%d" % ndma[0]
+        ndma[0] += 1
+        count[sem] = 16
+        QUEUE[q].dma_start(out, in_).then_inc(T.sem[sem], 16)
+        note(sem, 16, reads, writes)
+
+    def send(dst, out, in_, reads, sem):
+        depend("G", reads, [])
+        rid, pid, _ = topo.addr(dst)
+        m = topo.mask(core, dst)
+        count["left"] = count.get("left", 0) + len(topo.engines(core, dst))
+        g.remote_dma(out, in_, T.sem[sem], T.sem.left, pid, rid, m)
+
+    def ap(r):
+        return T[r[0]][:, r[1]:r[2]] if len(r) == 3 else T[r[0]][:, r[1]:r[2]:r[3]]
+
+    def apx(r):
+        return (ap(r[0]).indirect(ap(r[1])), [r[0], r[1]]) if not isinstance(r[0], str) else (ap(r), [r])
+
+    def tt(o, a, b, f):
+        x, rd = apx(a)
+        op("V", rd + [b], [o], lambda e: e.tensor_tensor(ap(o), x, ap(b), f))
+
+    def ts(o, a, s1, f1, s2=None, f2=None, q="V"):
+        x, rd = apx(a)
+        rd = list(rd)
+        if isinstance(s1, str):
+            rd.append((s1, 0, 1))
+            s1 = T[s1][:, 0:1]
+        if f2 is None: op(q, rd, [o], lambda e: e.tensor_scalar(ap(o), x, s1, None, f1))
+        else: op(q, rd, [o], lambda e: e.tensor_scalar(ap(o), x, s1, s2, f1, f2))
+
+    def cp(o, a):
+        x, rd = apx(a)
+        op("V", rd, [o], lambda e: e.tensor_copy(ap(o), x))
+
+    def ac(o, a, f=AF.Copy, scale=1.0, bias=0.0):
+        x, rd = apx(a)
+        rd = list(rd)
+        arg = {}
+        for n, s, plain in (("bias", bias, 0.0), ("scale", scale, 1.0)):
+            if isinstance(s, str):
+                rd.append((s, 0, 1))
+                arg[n] = T[s][:, 0:1]
+            elif s != plain: arg[n] = s
+        op("A", rd, [o], lambda e: e.activation(ap(o), x, f, **arg))
+
+    def move(q, o, a):
+        (cp if q == "V" else ac)(o, a)
+
+    def scaled(q, o, a, s):
+        if q == "V": ts(o, a, s, OP.mult)
+        else: ac(o, a, scale=s)
+
+    def scan(o, a, f=OP.max):
+        op("V", [("mask", 0, C), a], [o], lambda e: e.tensor_tensor_scan(ap(o), T.mask[:, 0:C], ap(a), 0.0, OP.mult, f))
+
+    def quant(q, s, lo, hi, a):
+        op("V", [a], [(q, lo, hi), (s, lo, hi)], lambda e: e.quantize_mx(T[q][:, lo:hi], T[s][:, lo:hi], ap(a)))
+
+    def mm(bank, n, w, ws, wlo, x, xs, lo):
+        op("P", [(w, wlo, wlo + 128), (ws, wlo, wlo + 128), (x, lo, lo + n), (xs, lo, lo + n)], [("ps", 512 * bank, 512 * bank + 512)],
+           lambda e: e.matmul_mx(T.ps[:, 512 * bank:512 * bank + n], T[w][:, wlo:wlo + 128], T[ws][:, wlo:wlo + 128], T[x][:, lo:lo + n], T[xs][:, lo:lo + n], True, True))
+
+    def psum(bank, n):
+        return ("ps", 512 * bank, 512 * bank + n)
+
+    def ends(b, i=0):
+        return (b, C * i + 15, C * i + C, 16)
+
+    def ports(o, s):
+        ts(o, s, "inv", OP.mult, -1.0, OP.add)
+
+    def wraps(o, s):
+        ac(o, s, AF.Identity, scale="inv", bias=-1.0)
+
+    def agents(o, s):
+        ts(o, s, "inv3", OP.mult, -2.0 / 3.0, OP.add)
+
+    dma("A", T.wlt[:, 0:72], T.wl[:, :], [], [("wlt", 0, 72)])
+    dma("S", T.ut[:, 0:512], T.u[:, :], [], [("ut", 0, 512)])
+    for i, (lo, hi) in enumerate(RUNS): dma("AS"[i], T.xt[:, 4 * lo:4 * hi], T.x[:, 4 * lo:4 * hi], [], [("xt", 4 * lo, 4 * hi)])
+    dma("S", T.wq[:, 0:512].bitcast(dt.uint8), T.wc[:, :], [], [("wq", 0, 512)])
+    dma("S", T.wp[:, 0:512], T.ws[:, :], [], [("wp", 0, 512)])
+    dma("S", T.vt[:, 0:512], T.v[:, :], [], [("vt", 0, 512)])
+
+    def iota(r, pattern, base, mult, flag):
+        op("G", [], [r], lambda e: e.iota(ap(r), pattern, base, mult, allow_small_or_imprecise_dtypes=True) if flag else e.iota(ap(r), pattern, base, mult))
+    iota(("pi32", 0, 1), [[0, 1]], 0, 1, False)
+    iota(("c48", 0, 24), [[48, 24]], 0, 0, True)
+    iota(("uoi", 0, 16), [[1, 2], [16, 8]], 0, 0, False)
+    iota(("jr", 0, 96), [[0, 6], [1, 16]], 0, 0, True)
+    side = 0 if rank < (rank ^ STEP[0]) else 1
+    op("V", [], [("ones", 0, F)], lambda e: e.memset(T.ones[:, 0:F], 1.0))
+    for j in range(3): ac(("acttab", j, F, 3), ("ones", 0, C), scale=-1e29 if j else 0.0)
+    ts(("p15i", 0, 1), ("pi32", 0, 1), 15, OP.bitwise_and)
+    cp(("p15", 0, 1), ("p15i", 0, 1))
+    ts(("np15", 0, 1), ("p15", 0, 1), -1.0, OP.mult)
+    ts(("np16", 0, 1), ("p15", 0, 1), -1.0, OP.mult, -1.0, OP.add)
+    ac(("e0", 0, 96), ("jr", 0, 96), AF.Sign, bias="np15")
+    ac(("e1", 0, 96), ("jr", 0, 96), AF.Abs, bias="np16")
+    ac(("e2", 0, 96), ("e0", 0, 96), AF.Abs)
+    ac(("e3", 0, 96), ("e1", 0, 96), AF.Relu, scale=-K, bias=K)
+    op("V", [("ones", 0, F)], [("idr", 0, F)], lambda e: e.tensor_tensor_scan(T.idr[:, 0:F], T.ones[:, 0:F], T.ones[:, 0:F], 0.0, OP.mult, OP.add))
+    op("G", [("ones", 0, 516)], [("eb", 0, 516)], lambda e: e.affine_select(T.eb[:, 0:516], T.ones[:, 0:516], [[-1, 516]], OP.is_equal, 0.0, 3, 4))
+    cp(("uo", 0, 16), ("uoi", 0, 16))
+    ts(("p3", 0, 1), ("p15", 0, 1), 3.0, OP.mult)
+    ts(("last", 0, 1), ("p15", 0, 1), 15.0, OP.is_equal)
+    ts(("c3", 0, 24), ("c48", 0, 24), "p3", OP.add)
+    ts(("inv", 0, 1), ("last", 0, 1), 1.0 - 1.0 / K, OP.mult, 1.0 / K, OP.add)
+    ts(("thp", 0, 1), ("last", 0, 1), 1.0 - K, OP.mult, K, OP.add)
+    ts(("inv3", 0, 1), ("inv", 0, 1), 1.0 / 3.0, OP.mult)
+    cp(("p0", 0, 24), ("c3", 0, 24))
+    tt(("mask", 0, 96), ("e2", 0, 96), ("e3", 0, 96), OP.max)
+    ac(("mask", 96, 192), ("mask", 0, 96))
+    ac(("mask", 192, C), ("mask", 0, 192))
+
+    w72 = ("wlt", 0, 72)
+    ts(("k1", 0, 72), w72, 384.0, OP.is_ge, -1151.0, OP.mult)
+    ts(("k2", 0, 72), w72, 768.0, OP.is_ge, -1151.0, OP.mult)
+    ts(("q3", 0, 72), w72, 3.0, OP.mult)
+    tt(("kk", 0, 72), ("k1", 0, 72), ("k2", 0, 72), OP.add)
+    tt(("k1", 0, 72), ("q3", 0, 72), ("kk", 0, 72), OP.add)
+    cp(("w16", 0, 72), ("k1", 0, 72))
+    move("A", ("om0", 1, F, 3), (("idr", 0, F), ("w16", 24, 48)))
+    move("A", ("om0", 2, F, 3), (("idr", 0, F), ("w16", 48, 72)))
+    move("V", ("om0", 0, F, 3), (("idr", 0, F), ("w16", 0, 24)))
+
+    W0, W1, W2 = ("u0", 0, 24), ("w12", 0, 24), ("w12", 24, 48)
+
+    def ready1(om, lst, loff, W0, W1, W2, meanwhile=None):
+        z = lambda n: (n, 0, 24)
+        ts(z("ai"), W0, 1.0 / 3.0, OP.mult, -1.0 / 3.0, OP.add)
+        tt(z("td"), W0, z("c3"), OP.subtract)
+        tt(z("ad0"), W2, W1, OP.subtract)
+        ts(z("a3"), z("ai"), 3.0, OP.mult)
+        tt(z("act"), W0, z("a3"), OP.is_equal)
+        if not meanwhile: move("A", ("thr", 0, C), (("acttab", 0, F), (lst, loff, loff + 24)))
+        tt(z("ta"), z("td"), z("act"), OP.mult)
+        tt(z("tau"), z("ta"), z("c3"), OP.add)
+        ts(("p0", 24, 48), z("tau"), 1.0, OP.add)
+        ts(("p0", 48, 72), z("tau"), 2.0, OP.add)
+        cp(("x12", 0, 48), ("p0", 24, 72))
+        if meanwhile: meanwhile()
+        ac(z("va"), z("act"), AF.Identity, scale=-1152.0, bias=1152.0)
+        ac(z("a2m"), z("act"), AF.Identity, scale=2.0, bias=-1.0)
+        move("A", ("y12", 0, C), ((om, 0, F), ("x12", 0, 24)))
+        move("A", ("y12", C, 2 * C), ((om, 0, F), ("x12", 24, 48)))
+        if meanwhile: move("A", ("thr", 0, C), (("acttab", 0, F), (lst, loff, loff + 24)))
+        tt(z("ad"), z("ad0"), z("act"), OP.mult)
+        tt(z("vta"), z("va"), z("tau"), OP.add)
+        tt(z("ss"), z("a2m"), z("ta"), OP.add)
+        ts(z("dst"), z("vta"), 1.0 / 3.0, OP.mult)
+        tt(("dp", 24, 48), z("a2m"), z("ta"), OP.subtract)
+        ac(("dp", 48, 72), z("ss"), AF.Identity, scale=-1.0, bias=-1.0)
+        tt(z("u10"), W1, z("ad"), OP.add)
+        tt(z("u12"), W2, z("ad"), OP.subtract)
+        tt(("du", 0, 24), z("u10"), W0, OP.subtract)
+
+    def ready2():
+        scan(("sy", 0, C), ("y12", 0, C))
+        scan(("sy", C, 2 * C), ("y12", C, 2 * C))
+        for j in range(2): wraps(("u0", 24 + 24 * j, 48 + 24 * j), ends("sy", j))
+
+    def quantx(lo, hi):
+        quant("xq", "xs", lo, hi, ("xt", 4 * lo, 4 * hi))
+
+    def scores(i):
+        lo, hi = RUNS[i]
+        mm(4 - 4 * i, hi - lo, "pq", "psc", 0, "xq", "xs", lo)
+        mm(5 - 4 * i, hi - lo, "pq", "psc", 128, "xq", "xs", lo)
+
+    def signs(i, q="V"):
+        lo, hi = RUNS[i]
+        n = hi - lo
+        if q == "V": ts(("ew", lo, hi), psum(4 - 4 * i, n), 0.0, OP.is_gt)
+        else:
+            op("A", [], [("sg", 0, n), psum(4 - 4 * i, n)], lambda e: e.activation(T.sg[:, 0:n], ap(psum(4 - 4 * i, n)), AF.Sign))
+            ac(("ew", lo, hi), ("sg", 0, n), AF.Relu)
+        ac(("ew", C + lo, C + hi), psum(5 - 4 * i, n), AF.Sign)
+        tt(("hrow", lo, hi), psum(4 - 4 * i, n), ("thr", lo, hi), OP.is_gt)
+
+    def halves(i):
+        lo, hi = RUNS[i]
+        for b in range(4): ac(("xh", C * b + lo, C * b + hi), ("xt", 4 * lo + b, 4 * hi, 4), scale=0.5)
+
+    def first():
+        quant("uq", "us", 0, 128, ("ut", 0, 512))
+        op("A", [("us", 0, 128), ("uo", 0, 16)], [("psc", 0, 256)], lambda e: e.activation(T.psc[:, 0:256], T.us[:, 0:128].indirect(T.uo[:, 0:16]), AF.Copy))
+        op("V", [("uq", 0, 128), ("uo", 0, 16)], [("pq", 0, 256)], lambda e: e.tensor_copy(T.pq[:, 0:256].bitcast(dt.uint32), T.uq[:, 0:128].bitcast(dt.uint32).indirect(T.uo[:, 0:16])))
+        for j in range(2): quant("em", "ems", 128 * j, 128 * j + 128, ("eb", 3 - 2 * side - j, 515 - 2 * side - j))
+        for lo, hi in RUNS: quantx(lo, hi)
+        scores(0)
+        scores(1)
+        mate = T.cores[rank ^ STEP[0]]
+        send(mate, T.el[:, 0:256].bitcast(dt.uint8), T.em[:, 0:256].bitcast(dt.uint8), [("em", 0, 256)], "ae")
+        send(mate, T.els[:, 0:256], T.ems[:, 0:256], [("ems", 0, 256)], "ae")
+        note("ae", 2 * len(topo.engines(core, mate)), [], [("el", 0, 256), ("els", 0, 256)])
+        for k in range(3): iota(("qtab", k, F, 3), [[1, C]], C * k, 0, True)
+        cp(W0, ("k1", 0, 24))
+
+    ready1("om0", "w16", 0, ("k1", 0, 24), ("k1", 24, 48), ("k1", 48, 72), first)
+    ready2()
+    signs(0)
+    tt(("du", 24, 48), W0, ("u0", 24, 48), OP.subtract)
+    tt(("du", 48, 72), ("u12", 0, 24), ("u0", 48, 72), OP.subtract)
+    signs(1)
+    halves(0)
+    halves(1)
+
+    for k in range(ROUNDS):
+        old, new = ("om0", "om1") if k % 2 == 0 else ("om1", "om0")
+        peer = T.cores[rank ^ STEP[k]]
+        dl, la, last = "dl%d" % k, "la%d" % k, k == ROUNDS - 1
+        tt(("fr", 0, C), (("ew", 0, 2 * C), ("dst", 0, 24)), ("hrow", 0, C), OP.is_equal)
+        scan(("fs", 0, C), ("fr", 0, C), OP.add)
+        z = lambda n: (n, 0, 72)
+        f = ("mp", 0, 24)
+        ts(f, ends("fs"), "thp", OP.is_ge)
+        for j in (1, 2): tt(("mp", 24 * j, 24 * j + 24), ("dp", 24 * j, 24 * j + 24), f, OP.mult)
+        tt(z("sp"), z("mp"), z("p0"), OP.add)
+        cp(z("p16"), z("sp"))
+        move("A", ("pir", 1, F, 3), (("idr", 0, F), ("p16", 24, 48)))
+        move("A", ("pir", 2, 866, 3), (("idr", 0, F), ("p16", 48, 66)))
+        for j in range(3): tt(("mu", 24 * j, 24 * j + 24), ("du", 24 * j, 24 * j + 24), f, OP.mult)
+        tt(z("su"), z("mu"), z("u0"), OP.add)
+        cp(z("u16"), z("su"))
+        move("V", ("pir", 0, F, 3), (("idr", 0, F), ("p16", 0, 24)))
+        move("V", ("pir", 866, F, 3), (("idr", 0, F), ("p16", 66, 72)))
+        for q, j in (("V", 1), ("A", 0), ("A", 2)): move(q, (new, j, F, 3), (("pir", 0, F), ("u16", 24 * j, 24 * j + 24)))
+        scan(("sc", C, 2 * C), (new, 1, F, 3))
+        agents(("l12", 0, 24), ends("sc", 1))
+        scan(("sc", 0, C), (new, 0, F, 3))
+        ports((dl, 0, 24), ends("sc", 0))
+        scan(("sc", 2 * C, 3 * C), (new, 2, F, 3))
+        agents(("l12", 24, 48), ends("sc", 2))
+        send(peer, T[la][:, 0:24], T[dl][:, 0:24], [(dl, 0, 24)], "al%d" % k)
+        note("al%d" % k, len(topo.engines(core, peer)), [], [(la, 0, 24)])
+        for i, (lo, hi) in enumerate(ZRUNS):
+            for b in range(4): move("A", ("gz", C * b + lo, C * b + hi), (("xh", C * b, C * b + C), ("l12", lo // 16, hi // 16)))
+        if not last:
+            for j, w in enumerate((W0, W1, W2)): wraps(w, ends("sc", j))
+        for i, (lo, hi) in enumerate(ZRUNS):
+            for b in range(4): tt(("zt", 4 * lo + b, 4 * hi, 4), (("xh", C * b, C * b + C), ("l12", 24 + lo // 16, 24 + hi // 16)), ("gz", C * b + lo, C * b + hi), OP.add)
+            quant("zq", "zs", lo, hi, ("zt", 4 * lo, 4 * hi))
+            for b in range(4): mm(4 * i + b, hi - lo, "wq", "wp", 128 * b, "zq", "zs", lo)
+        def look():
+            move("A", ("mr", 0, C), ((new, 0, F), (la, 0, 24)))
+
+        def places():
+            scan(("ms", 0, C), ("mr", 0, C))
+            agents(("ml", 0, 24), ends("ms"))
+        for n, (q, i, b) in enumerate((("A", 0, 0), ("A", 0, 1), ("V", 0, 2), ("A", 0, 3), ("V", 1, 0), ("A", 1, 1), ("V", 1, 2), ("A", 1, 3))):
+            if n == 1: look()
+            if n == 3: places()
+            lo, hi = ZRUNS[i]
+            scaled(q, ("hp", C * b + lo, C * b + hi), psum(4 * i + b, hi - lo), 0.03125)
+        hq, hs, lq, ls = "hq%d" % k, "hs%d" % k, "lq%d" % k, "ls%d" % k
+        for i, (lo, hi) in enumerate(EXCHANGE[k]):
+            for q, b in (("V", 0), ("A", 1), ("V", 2), ("A", 3)):
+                move(q, ("hg", 4 * lo + b, 4 * hi, 4), (("hp", C * b, C * b + C), ("ml", lo // 16, hi // 16)))
+            quant(hq, hs, lo, hi, ("hg", 4 * lo, 4 * hi))
+            send(peer, T[lq][:, lo:hi].bitcast(dt.uint8), T[hq][:, lo:hi].bitcast(dt.uint8), [(hq, lo, hi)], "ah%d%d" % (k, i))
+            send(peer, T[ls][:, lo:hi], T[hs][:, lo:hi], [(hs, lo, hi)], "ah%d%d" % (k, i))
+            note("ah%d%d" % (k, i), 2 * len(topo.engines(core, peer)), [], [(lq, lo, hi), (ls, lo, hi)])
+        if k == 1: quant("vq", "vs", 0, 128, ("vt", 0, 512))
+        if not last:
+            ready1(new, dl, 0, W0, W1, W2)
+            ready2()
+        else:
+            for j in range(3): ports(("fin", 24 * j, 24 * j + 24), ends("sc", j))
+            move("A", ("owr", 0, F), (("qtab", 0, F), ("fin", 0, 72)))
+            for j in range(8): dma("S", T.ow[j:j + 1, :], T.owr[16 * j:16 * j + 1, 0:F], [("owr", 0, F)], [])
+        def unpack(i):
+            lo, hi = EXCHANGE[k][i]
+            for b in range(4):
+                e, es = ("em", "ems") if b // 2 == side else ("el", "els")
+                mm(4 - 4 * (i % 2) + b, hi - lo, e, es, 128 * (b % 2), lq, ls, lo)
+
+        def add(i):
+            lo, hi = EXCHANGE[k][i]
+            for b in range(4):
+                x = ("xt", 4 * lo + b, 4 * hi, 4)
+                tt(x, psum(4 - 4 * (i % 2) + b, hi - lo), x, OP.add)
+            quantx(lo, hi)
+
+        def store(bank, lo, hi):
+            mm(bank, hi - lo, "vq", "vs", 0, "xq", "xs", lo)
+            dma("S", T.oc[:, 4 * lo:4 * hi], T.xq[:, lo:hi].bitcast(dt.uint8), [("xq", lo, hi)], [])
+            for j in range(4): dma("A" if j % 2 else "S", T.osc[4 * j:4 * j + 4, lo:hi], T.xs[32 * j:32 * j + 4, lo:hi], [("xs", lo, hi)], [])
+            ac(("yt", lo, hi), psum(bank, hi - lo))
+            dma("A", T.y[:, lo:hi], T.yt[:, lo:hi], [("yt", lo, hi)], [])
+        unpack(0)
+        unpack(1)
+        add(0)
+        if not last:
+            scores(0)
+            tt(("du", 24, 48), W0, ("u0", 24, 48), OP.subtract)
+            tt(("du", 48, 72), ("u12", 0, 24), ("u0", 48, 72), OP.subtract)
+            halves(0)
+            add(1)
+            scores(1)
+            signs(0, "A")
+            signs(1)
+            halves(1)
+        else:
+            unpack(2)
+            add(1)
+            store(0, 0, 256)
+            add(2)
+            store(1, 256, 384)
+    for sem in ("V", "A", "P", "G", "left"): wait("G", sem, count[sem])
+    for j in range(ndma[0]): wait("G", "d%d" % j, 16)

@@ -4,52 +4,45 @@ OP = AluOpType
 C = 384
 F = 3 * C
 K = 4194304.0
+SMALL = 1.0 / 2048
 ROUNDS = 3
 STEP = [1, 2, 3]
 RUNS = [(0, 192), (192, 384)]
 EXCHANGE = [RUNS, RUNS, [(0, 128), (128, 256), (256, 384)]]
 ZRUNS = [(0, 256), (256, 384)]
+EVACUATE = ["AAVA", "VVVV"]
+PICK = [["AAVV", "AAAV"], ["AAVV", "AAAV"], ["AAVV", "AAVV", "AAAV"]]
+P0, P1, U0, U2, U1 = range(5)
 
 SCRATCH = {
     "xt": ("sbuf", [128, 4 * C], "bfloat16"), "xh": ("sbuf", [128, 4 * C], "bfloat16"), "gz": ("sbuf", [128, 4 * C], "bfloat16"),
     "zt": ("sbuf", [128, 4 * C], "bfloat16"), "hp": ("sbuf", [128, 4 * C], "bfloat16"), "hg": ("sbuf", [128, 4 * C], "bfloat16"),
     "ut": ("sbuf", [128, 512], "bfloat16"), "vt": ("sbuf", [128, 512], "bfloat16"),
-    "ones": ("sbuf", [128, F], "bfloat16"), "eb": ("sbuf", [128, 516], "bfloat16"),
+    "ones": ("sbuf", [128, 516], "bfloat16"), "eb": ("sbuf", [128, 516], "bfloat16"),
     "uq": ("sbuf", [128, 128], "float8_e4m3fn_x4"), "us": ("sbuf", [128, 128], "uint8"),
     "pq": ("sbuf", [128, 256], "float8_e4m3fn_x4"), "psc": ("sbuf", [128, 256], "uint8"),
     "vq": ("sbuf", [128, 128], "float8_e4m3fn_x4"), "vs": ("sbuf", [128, 128], "uint8"),
     "em": ("sbuf", [128, 256], "float8_e4m3fn_x4"), "ems": ("sbuf", [128, 256], "uint8"), "el": ("sbuf", [128, 256], "float8_e4m3fn_x4"), "els": ("sbuf", [128, 256], "uint8"),
-    "sg": ("sbuf", [128, 192], "float32"),
     "wq": ("sbuf", [128, 512], "float8_e4m3fn_x4"), "wp": ("sbuf", [128, 512], "uint8"),
     "xq": ("sbuf", [128, C], "float8_e4m3fn_x4"), "xs": ("sbuf", [128, C], "uint8"),
     "zq": ("sbuf", [128, C], "float8_e4m3fn_x4"), "zs": ("sbuf", [128, C], "uint8"),
-    "wlt": ("sbuf", [128, 72], "int32"), "pi32": ("sbuf", [128, 1], "int32"), "p15i": ("sbuf", [128, 1], "int32"),
-    "p15": ("sbuf", [128, 1], "float32"), "p3": ("sbuf", [128, 1], "float32"), "last": ("sbuf", [128, 1], "float32"),
-    "inv": ("sbuf", [128, 1], "float32"), "inv3": ("sbuf", [128, 1], "float32"), "thp": ("sbuf", [128, 1], "float32"),
-    "c48": ("sbuf", [128, 24], "float32"), "c3": ("sbuf", [128, 24], "float32"),
+    "wlt": ("sbuf", [128, 72], "int32"), "wl16": ("sbuf", [128, 72], "uint16"), "pi32": ("sbuf", [128, 1], "int32"), "p15i": ("sbuf", [128, 1], "int32"),
     "uoi": ("sbuf", [128, 16], "int32"), "uo": ("sbuf", [128, 16], "uint16"),
-    "np15": ("sbuf", [128, 1], "float32"), "np16": ("sbuf", [128, 1], "float32"),
-    "jr": ("sbuf", [128, 96], "float32"), "e0": ("sbuf", [128, 96], "float32"), "e1": ("sbuf", [128, 96], "float32"), "e2": ("sbuf", [128, 96], "float32"), "e3": ("sbuf", [128, 96], "float32"), "mask": ("sbuf", [128, C], "float32"),
-    "idr": ("sbuf", [128, F], "float32"), "qtab": ("sbuf", [128, F], "float32"), "acttab": ("sbuf", [128, F], "bfloat16"),
+    "mk": ("sbuf", [128, C], "bfloat16"), "mn": ("sbuf", [128, C], "bfloat16"),
+    "idr": ("sbuf", [128, F], "float32"), "t2": ("sbuf", [128, F], "float32"), "qtab": ("sbuf", [128, F], "float32"),
     "pir": ("sbuf", [128, F], "float32"), "om0": ("sbuf", [128, F], "float32"), "om1": ("sbuf", [128, F], "float32"),
-    "ew": ("sbuf", [128, 2 * C], "float32"), "hrow": ("sbuf", [128, C], "float32"), "thr": ("sbuf", [128, C], "float32"),
-    "fr": ("sbuf", [128, C], "float32"), "fs": ("sbuf", [128, C], "float32"),
-    "sc": ("sbuf", [128, F], "float32"), "y12": ("sbuf", [128, 2 * C], "float32"), "sy": ("sbuf", [128, 2 * C], "float32"),
-    "mr": ("sbuf", [128, C], "float32"), "ms": ("sbuf", [128, C], "float32"), "ml": ("sbuf", [128, 24], "uint16"),
-    "l12": ("sbuf", [128, 48], "uint16"),
-    "q3": ("sbuf", [128, 72], "float32"), "k1": ("sbuf", [128, 72], "float32"), "k2": ("sbuf", [128, 72], "float32"), "kk": ("sbuf", [128, 72], "float32"),
-    "u0": ("sbuf", [128, 72], "float32"), "du": ("sbuf", [128, 72], "float32"), "w12": ("sbuf", [128, 48], "float32"),
-    "p0": ("sbuf", [128, 72], "float32"), "dp": ("sbuf", [128, 72], "float32"),
-    "mp": ("sbuf", [128, 72], "float32"), "sp": ("sbuf", [128, 72], "float32"), "p16": ("sbuf", [128, 72], "uint16"),
-    "mu": ("sbuf", [128, 72], "float32"), "su": ("sbuf", [128, 72], "float32"), "u16": ("sbuf", [128, 72], "uint16"),
-    "ai": ("sbuf", [128, 24], "int32"), "a3": ("sbuf", [128, 24], "float32"), "act": ("sbuf", [128, 24], "float32"),
-    "td": ("sbuf", [128, 24], "float32"), "ta": ("sbuf", [128, 24], "float32"), "tau": ("sbuf", [128, 24], "float32"),
-    "ad0": ("sbuf", [128, 24], "float32"), "ad": ("sbuf", [128, 24], "float32"), "x12": ("sbuf", [128, 48], "uint16"),
-    "a2m": ("sbuf", [128, 24], "float32"), "va": ("sbuf", [128, 24], "float32"), "vta": ("sbuf", [128, 24], "float32"), "ss": ("sbuf", [128, 24], "float32"),
-    "u10": ("sbuf", [128, 24], "float32"), "u12": ("sbuf", [128, 24], "float32"), "dst": ("sbuf", [128, 24], "uint16"),
-    "w16": ("sbuf", [128, 72], "uint16"), "fin": ("sbuf", [128, 72], "uint16"), "owr": ("sbuf", [128, F], "float32"), "yt": ("sbuf", [128, C], "float32"),
+    "ew": ("sbuf", [128, 2 * C], "bfloat16"), "gr": ("sbuf", [128, C], "bfloat16"), "gs": ("sbuf", [128, C], "bfloat16"), "aw": ("sbuf", [128, C], "bfloat16"),
+    "cb": ("sbuf", [128, 240], "float32"), "ca": ("sbuf", [128, 240], "float32"), "co": ("sbuf", [128, 240], "float32"), "l16": ("sbuf", [128, 120], "uint16"),
+    "sc": ("sbuf", [128, F], "float32"), "y12": ("sbuf", [128, 2 * C], "float16"), "sy": ("sbuf", [128, 2 * C], "float16"),
+    "mr": ("sbuf", [128, C], "float16"), "ms": ("sbuf", [128, C], "float16"), "ml": ("sbuf", [128, 24], "uint16"),
+    "l12": ("sbuf", [128, 48], "uint16"), "x12": ("sbuf", [128, 48], "uint16"), "w": ("sbuf", [128, 96], "float32"),
+    "wi": ("sbuf", [128, 24], "int32"), "dst": ("sbuf", [128, 24], "uint16"),
+    "fin": ("sbuf", [128, 72], "uint16"), "owr": ("sbuf", [128, F], "float32"), "yt": ("sbuf", [128, C], "float32"),
     "ps": ("psum", [128, 4096], "float32"),
 }
+for _n in ("p15", "p16", "p3", "last", "inv", "inv3", "thp"): SCRATCH[_n] = ("sbuf", [128, 1], "float32")
+for _n in ("c48", "c3", "c31", "act", "td", "ta", "ad0", "ad", "a2m", "va", "vta", "u10", "hw", "ink", "q3"): SCRATCH[_n] = ("sbuf", [128, 24], "float32")
+for _n in ("jr", "e0", "e1", "e2", "e3"): SCRATCH[_n] = ("sbuf", [128, 96], "bfloat16")
 for _k in range(ROUNDS):
     SCRATCH["dl%d" % _k] = ("sbuf", [128, 24], "uint16")
     SCRATCH["la%d" % _k] = ("sbuf", [128, 24], "uint16")
@@ -128,18 +121,20 @@ def rank_program(g, core, T, topo):
     def apx(r):
         return (ap(r[0]).indirect(ap(r[1])), [r[0], r[1]]) if not isinstance(r[0], str) else (ap(r), [r])
 
+    def column(s, rd):
+        if not isinstance(s, str): return s
+        rd.append((s, 0, 1))
+        return T[s][:, 0:1]
+
     def tt(o, a, b, f):
         x, rd = apx(a)
         op("V", rd + [b], [o], lambda e: e.tensor_tensor(ap(o), x, ap(b), f))
 
-    def ts(o, a, s1, f1, s2=None, f2=None, q="V"):
+    def ts(o, a, s1, f1, s2=None, f2=None):
         x, rd = apx(a)
-        rd = list(rd)
-        if isinstance(s1, str):
-            rd.append((s1, 0, 1))
-            s1 = T[s1][:, 0:1]
-        if f2 is None: op(q, rd, [o], lambda e: e.tensor_scalar(ap(o), x, s1, None, f1))
-        else: op(q, rd, [o], lambda e: e.tensor_scalar(ap(o), x, s1, s2, f1, f2))
+        s1, s2 = column(s1, rd), column(s2, rd)
+        if f2 is None: op("V", rd, [o], lambda e: e.tensor_scalar(ap(o), x, s1, None, f1))
+        else: op("V", rd, [o], lambda e: e.tensor_scalar(ap(o), x, s1, s2, f1, f2))
 
     def cp(o, a):
         x, rd = apx(a)
@@ -147,14 +142,14 @@ def rank_program(g, core, T, topo):
 
     def ac(o, a, f=AF.Copy, scale=1.0, bias=0.0):
         x, rd = apx(a)
-        rd = list(rd)
-        arg = {}
-        for n, s, plain in (("bias", bias, 0.0), ("scale", scale, 1.0)):
-            if isinstance(s, str):
-                rd.append((s, 0, 1))
-                arg[n] = T[s][:, 0:1]
-            elif s != plain: arg[n] = s
+        arg = {n: column(s, rd) for n, s, plain in (("bias", bias, 0.0), ("scale", scale, 1.0)) if s != plain}
         op("A", rd, [o], lambda e: e.activation(ap(o), x, f, **arg))
+
+    def lin(o, a, scale, bias):
+        ac(o, a, AF.Identity, scale=scale, bias=bias)
+
+    def fill(o, v):
+        op("V", [], [o], lambda e: e.memset(ap(o), v))
 
     def move(q, o, a):
         (cp if q == "V" else ac)(o, a)
@@ -163,8 +158,11 @@ def rank_program(g, core, T, topo):
         if q == "V": ts(o, a, s, OP.mult)
         else: ac(o, a, scale=s)
 
-    def scan(o, a, f=OP.max):
-        op("V", [("mask", 0, C), a], [o], lambda e: e.tensor_tensor_scan(ap(o), T.mask[:, 0:C], ap(a), 0.0, OP.mult, f))
+    def scan(o, d0, d1, first, f):
+        op("V", [d0, d1], [o], lambda e: e.tensor_tensor_scan(ap(o), ap(d0), ap(d1), first, OP.mult, f))
+
+    def wrap(o, a):
+        scan(o, ("mn", 0, C), a, 1.0, OP.min)
 
     def quant(q, s, lo, hi, a):
         op("V", [a], [(q, lo, hi), (s, lo, hi)], lambda e: e.quantize_mx(T[q][:, lo:hi], T[s][:, lo:hi], ap(a)))
@@ -176,17 +174,26 @@ def rank_program(g, core, T, topo):
     def psum(bank, n):
         return ("ps", 512 * bank, 512 * bank + n)
 
-    def ends(b, i=0):
-        return (b, C * i + 15, C * i + C, 16)
+    def z(n):
+        return (n, 0, 24)
+
+    def ends(b, i=0, n=1):
+        return (b, C * i + 15, C * (i + n), 16)
 
     def ports(o, s):
         ts(o, s, "inv", OP.mult, -1.0, OP.add)
 
-    def wraps(o, s):
-        ac(o, s, AF.Identity, scale="inv", bias=-1.0)
-
     def agents(o, s):
         ts(o, s, "inv3", OP.mult, -2.0 / 3.0, OP.add)
+
+    def value(i, n=1):
+        return ("ca", 48 * i + 1, 48 * (i + n), 2)
+
+    def diff(i, n=1):
+        return ("cb", 48 * i + 1, 48 * (i + n), 2)
+
+    def chosen(i, lo=0, hi=C):
+        return ("l16", 24 * i + lo // 16, 24 * i + hi // 16)
 
     dma("A", T.wlt[:, 0:72], T.wl[:, :], [], [("wlt", 0, 72)])
     dma("S", T.ut[:, 0:512], T.u[:, :], [], [("ut", 0, 512)])
@@ -198,188 +205,204 @@ def rank_program(g, core, T, topo):
     def iota(r, pattern, base, mult, flag):
         op("G", [], [r], lambda e: e.iota(ap(r), pattern, base, mult, allow_small_or_imprecise_dtypes=True) if flag else e.iota(ap(r), pattern, base, mult))
     iota(("pi32", 0, 1), [[0, 1]], 0, 1, False)
+    iota(("jr", 0, 96), [[0, 6], [1, 16]], 0, 0, True)
     iota(("c48", 0, 24), [[48, 24]], 0, 0, True)
     iota(("uoi", 0, 16), [[1, 2], [16, 8]], 0, 0, False)
-    iota(("jr", 0, 96), [[0, 6], [1, 16]], 0, 0, True)
     side = 0 if rank < (rank ^ STEP[0]) else 1
-    op("V", [], [("ones", 0, F)], lambda e: e.memset(T.ones[:, 0:F], 1.0))
-    for j in range(3): ac(("acttab", j, F, 3), ("ones", 0, C), scale=-1e29 if j else 0.0)
+    fill(("ones", 0, 516), 1.0)
     ts(("p15i", 0, 1), ("pi32", 0, 1), 15, OP.bitwise_and)
+    fill(("cb", 0, 240), 0.0)
     cp(("p15", 0, 1), ("p15i", 0, 1))
-    ts(("np15", 0, 1), ("p15", 0, 1), -1.0, OP.mult)
-    ts(("np16", 0, 1), ("p15", 0, 1), -1.0, OP.mult, -1.0, OP.add)
-    ac(("e0", 0, 96), ("jr", 0, 96), AF.Sign, bias="np15")
-    ac(("e1", 0, 96), ("jr", 0, 96), AF.Abs, bias="np16")
-    ac(("e2", 0, 96), ("e0", 0, 96), AF.Abs)
-    ac(("e3", 0, 96), ("e1", 0, 96), AF.Relu, scale=-K, bias=K)
-    op("V", [("ones", 0, F)], [("idr", 0, F)], lambda e: e.tensor_tensor_scan(T.idr[:, 0:F], T.ones[:, 0:F], T.ones[:, 0:F], 0.0, OP.mult, OP.add))
+    fill(diff(P0), 1.0)
+    iota(("idr", 2, F, 3), [[3, C]], 3, 0, True)
     op("G", [("ones", 0, 516)], [("eb", 0, 516)], lambda e: e.affine_select(T.eb[:, 0:516], T.ones[:, 0:516], [[-1, 516]], OP.is_equal, 0.0, 3, 4))
-    cp(("uo", 0, 16), ("uoi", 0, 16))
+    for j in range(2): iota(("t2", j, F, 3), [[3, C]], 3, 0, True)
+    ts(("p16", 0, 1), ("p15", 0, 1), 1.0, OP.add)
     ts(("p3", 0, 1), ("p15", 0, 1), 3.0, OP.mult)
     ts(("last", 0, 1), ("p15", 0, 1), 15.0, OP.is_equal)
-    ts(("c3", 0, 24), ("c48", 0, 24), "p3", OP.add)
-    ts(("inv", 0, 1), ("last", 0, 1), 1.0 - 1.0 / K, OP.mult, 1.0 / K, OP.add)
+    j96 = ("jr", 0, 96)
+    ts(("e0", 0, 96), j96, "p15", OP.not_equal)
+    ts(("e1", 0, 96), j96, "p16", OP.is_equal, K, OP.mult)
+    ts(("e2", 0, 96), j96, "p15", OP.is_equal, K, OP.mult)
+    ts(("e3", 0, 96), j96, "p16", OP.not_equal, SMALL, OP.max)
+    ts(z("c3"), z("c48"), "p3", OP.add)
+    ts(z("c31"), z("c48"), "p3", OP.add, 1.0, OP.add)
+    ts(value(P0), z("c48"), "p3", OP.add)
+    ts(value(U0), z("c48"), "p3", OP.add)
+    tt(("mk", 0, 96), ("e0", 0, 96), ("e1", 0, 96), OP.max)
+    tt(("mn", 0, 96), ("e2", 0, 96), ("e3", 0, 96), OP.max)
+    ts(("inv", 0, 1), ("last", 0, 1), 1.0 - 1.0 / SMALL, OP.mult, 1.0 / SMALL, OP.add)
+    ts(("inv3", 0, 1), ("last", 0, 1), (1.0 - 1.0 / SMALL) / 3.0, OP.mult, 1.0 / SMALL / 3.0, OP.add)
     ts(("thp", 0, 1), ("last", 0, 1), 1.0 - K, OP.mult, K, OP.add)
-    ts(("inv3", 0, 1), ("inv", 0, 1), 1.0 / 3.0, OP.mult)
-    cp(("p0", 0, 24), ("c3", 0, 24))
-    tt(("mask", 0, 96), ("e2", 0, 96), ("e3", 0, 96), OP.max)
-    ac(("mask", 96, 192), ("mask", 0, 96))
-    ac(("mask", 192, C), ("mask", 0, 192))
+    cp(("uo", 0, 16), ("uoi", 0, 16))
+    for lo in (96, 192):
+        for m in ("mk", "mn"): cp((m, lo, 2 * lo), (m, 0, lo))
+    for j, b in ((0, -1.875), (1, -1.0)): lin(("idr", j, F, 3), ("idr", 2, F, 3), 1.0, b)
 
-    w72 = ("wlt", 0, 72)
-    ts(("k1", 0, 72), w72, 384.0, OP.is_ge, -1151.0, OP.mult)
-    ts(("k2", 0, 72), w72, 768.0, OP.is_ge, -1151.0, OP.mult)
-    ts(("q3", 0, 72), w72, 3.0, OP.mult)
-    tt(("kk", 0, 72), ("k1", 0, 72), ("k2", 0, 72), OP.add)
-    tt(("k1", 0, 72), ("q3", 0, 72), ("kk", 0, 72), OP.add)
-    cp(("w16", 0, 72), ("k1", 0, 72))
-    move("A", ("om0", 1, F, 3), (("idr", 0, F), ("w16", 24, 48)))
-    move("A", ("om0", 2, F, 3), (("idr", 0, F), ("w16", 48, 72)))
-    move("V", ("om0", 0, F, 3), (("idr", 0, F), ("w16", 0, 24)))
+    W0, W1, W2 = ("w", 24, 48), ("w", 48, 72), ("w", 72, 96)
 
-    W0, W1, W2 = ("u0", 0, 24), ("w12", 0, 24), ("w12", 24, 48)
+    def flags():
+        lin(z("va"), z("act"), -1152.0, 1151.0)
+        lin(z("a2m"), z("act"), 2.0, -1.0)
+        lin(z("ink"), z("act"), -2.0 * K, "thp")
 
-    def ready1(om, lst, loff, W0, W1, W2, meanwhile=None):
-        z = lambda n: (n, 0, 24)
-        ts(z("ai"), W0, 1.0 / 3.0, OP.mult, -1.0 / 3.0, OP.add)
-        tt(z("td"), W0, z("c3"), OP.subtract)
-        tt(z("ad0"), W2, W1, OP.subtract)
-        ts(z("a3"), z("ai"), 3.0, OP.mult)
-        tt(z("act"), W0, z("a3"), OP.is_equal)
-        if not meanwhile: move("A", ("thr", 0, C), (("acttab", 0, F), (lst, loff, loff + 24)))
+    def principal():
         tt(z("ta"), z("td"), z("act"), OP.mult)
-        tt(z("tau"), z("ta"), z("c3"), OP.add)
-        ts(("p0", 24, 48), z("tau"), 1.0, OP.add)
-        ts(("p0", 48, 72), z("tau"), 2.0, OP.add)
-        cp(("x12", 0, 48), ("p0", 24, 72))
-        if meanwhile: meanwhile()
-        ac(z("va"), z("act"), AF.Identity, scale=-1152.0, bias=1152.0)
-        ac(z("a2m"), z("act"), AF.Identity, scale=2.0, bias=-1.0)
-        move("A", ("y12", 0, C), ((om, 0, F), ("x12", 0, 24)))
-        move("A", ("y12", C, 2 * C), ((om, 0, F), ("x12", 24, 48)))
-        if meanwhile: move("A", ("thr", 0, C), (("acttab", 0, F), (lst, loff, loff + 24)))
-        tt(z("ad"), z("ad0"), z("act"), OP.mult)
-        tt(z("vta"), z("va"), z("tau"), OP.add)
-        tt(z("ss"), z("a2m"), z("ta"), OP.add)
-        ts(z("dst"), z("vta"), 1.0 / 3.0, OP.mult)
-        tt(("dp", 24, 48), z("a2m"), z("ta"), OP.subtract)
-        ac(("dp", 48, 72), z("ss"), AF.Identity, scale=-1.0, bias=-1.0)
-        tt(z("u10"), W1, z("ad"), OP.add)
-        tt(z("u12"), W2, z("ad"), OP.subtract)
-        tt(("du", 0, 24), z("u10"), W0, OP.subtract)
+        tt(value(P1), z("ta"), z("c31"), OP.add)
 
-    def ready2():
-        scan(("sy", 0, C), ("y12", 0, C))
-        scan(("sy", C, 2 * C), ("y12", C, 2 * C))
-        for j in range(2): wraps(("u0", 24 + 24 * j, 48 + 24 * j), ends("sy", j))
+    def deciding():
+        tt(z("vta"), z("va"), value(P1), OP.add)
+        tt(diff(P1), z("a2m"), z("ta"), OP.subtract)
+        ts(z("dst"), z("vta"), 1.0 / 3.0, OP.mult)
 
     def quantx(lo, hi):
         quant("xq", "xs", lo, hi, ("xt", 4 * lo, 4 * hi))
 
     def scores(i):
         lo, hi = RUNS[i]
-        mm(4 - 4 * i, hi - lo, "pq", "psc", 0, "xq", "xs", lo)
         mm(5 - 4 * i, hi - lo, "pq", "psc", 128, "xq", "xs", lo)
+        mm(4 - 4 * i, hi - lo, "pq", "psc", 0, "xq", "xs", lo)
 
-    def signs(i, q="V"):
+    def sign_a(i):
         lo, hi = RUNS[i]
-        n = hi - lo
-        if q == "V": ts(("ew", lo, hi), psum(4 - 4 * i, n), 0.0, OP.is_gt)
-        else:
-            op("A", [], [("sg", 0, n), psum(4 - 4 * i, n)], lambda e: e.activation(T.sg[:, 0:n], ap(psum(4 - 4 * i, n)), AF.Sign))
-            ac(("ew", lo, hi), ("sg", 0, n), AF.Relu)
-        ac(("ew", C + lo, C + hi), psum(5 - 4 * i, n), AF.Sign)
-        tt(("hrow", lo, hi), psum(4 - 4 * i, n), ("thr", lo, hi), OP.is_gt)
+        ts(("ew", lo, hi), psum(4 - 4 * i, hi - lo), 0.0, OP.is_gt, 0.5, OP.subtract)
+
+    def sign_b(i):
+        lo, hi = RUNS[i]
+        ac(("ew", C + lo, C + hi), psum(5 - 4 * i, hi - lo), AF.Sign)
+
+    def wrap_a(i):
+        lo, hi = RUNS[i]
+        scan(("aw", lo, hi), ("mk", lo, hi), ("ew", lo, hi), 0.0, OP.add)
 
     def halves(i):
         lo, hi = RUNS[i]
         for b in range(4): ac(("xh", C * b + lo, C * b + hi), ("xt", 4 * lo + b, 4 * hi, 4), scale=0.5)
 
-    def first():
-        quant("uq", "us", 0, 128, ("ut", 0, 512))
-        op("A", [("us", 0, 128), ("uo", 0, 16)], [("psc", 0, 256)], lambda e: e.activation(T.psc[:, 0:256], T.us[:, 0:128].indirect(T.uo[:, 0:16]), AF.Copy))
-        op("V", [("uq", 0, 128), ("uo", 0, 16)], [("pq", 0, 256)], lambda e: e.tensor_copy(T.pq[:, 0:256].bitcast(dt.uint32), T.uq[:, 0:128].bitcast(dt.uint32).indirect(T.uo[:, 0:16])))
-        for j in range(2): quant("em", "ems", 128 * j, 128 * j + 128, ("eb", 3 - 2 * side - j, 515 - 2 * side - j))
-        for lo, hi in RUNS: quantx(lo, hi)
-        scores(0)
-        scores(1)
-        mate = T.cores[rank ^ STEP[0]]
-        send(mate, T.el[:, 0:256].bitcast(dt.uint8), T.em[:, 0:256].bitcast(dt.uint8), [("em", 0, 256)], "ae")
-        send(mate, T.els[:, 0:256], T.ems[:, 0:256], [("ems", 0, 256)], "ae")
-        note("ae", 2 * len(topo.engines(core, mate)), [], [("el", 0, 256), ("els", 0, 256)])
-        for k in range(3): iota(("qtab", k, F, 3), [[1, C]], C * k, 0, True)
-        cp(W0, ("k1", 0, 24))
-
-    ready1("om0", "w16", 0, ("k1", 0, 24), ("k1", 24, 48), ("k1", 48, 72), first)
-    ready2()
-    signs(0)
-    tt(("du", 24, 48), W0, ("u0", 24, 48), OP.subtract)
-    tt(("du", 48, 72), ("u12", 0, 24), ("u0", 48, 72), OP.subtract)
-    signs(1)
+    w0 = ("wlt", 0, 24)
+    ts(z("act"), w0, float(C), OP.is_lt)
+    ts(z("q3"), w0, 3.0, OP.mult)
+    cp(("wl16", 0, 72), ("wlt", 0, 72))
+    tt(z("td"), z("q3"), z("c3"), OP.subtract)
+    quant("uq", "us", 0, 128, ("ut", 0, 512))
+    flags()
+    principal()
+    op("A", [("us", 0, 128), ("uo", 0, 16)], [("psc", 0, 256)], lambda e: e.activation(T.psc[:, 0:256], T.us[:, 0:128].indirect(T.uo[:, 0:16]), AF.Copy))
+    op("V", [("uq", 0, 128), ("uo", 0, 16)], [("pq", 0, 256)], lambda e: e.tensor_copy(T.pq[:, 0:256].bitcast(dt.uint32), T.uq[:, 0:128].bitcast(dt.uint32).indirect(T.uo[:, 0:16])))
+    deciding()
+    for j in range(2): quant("em", "ems", 128 * j, 128 * j + 128, ("eb", 3 - 2 * side - j, 515 - 2 * side - j))
+    for lo, hi in RUNS: quantx(lo, hi)
+    scores(0)
+    scores(1)
+    mate = T.cores[rank ^ STEP[0]]
+    send(mate, T.el[:, 0:256].bitcast(dt.uint8), T.em[:, 0:256].bitcast(dt.uint8), [("em", 0, 256)], "ae")
+    send(mate, T.els[:, 0:256], T.ems[:, 0:256], [("ems", 0, 256)], "ae")
+    note("ae", 2 * len(topo.engines(core, mate)), [], [("el", 0, 256), ("els", 0, 256)])
+    ac(("t2", 2, F, 3), ("idr", 0, F, 3))
     halves(0)
-    halves(1)
+    ts(diff(U0), z("act"), 1.0, OP.add)
+    cp(value(U1), value(P1))
+    ts(value(U2), value(P1), 1.0, OP.add)
+    ts(diff(U1), z("ta"), -1.0, OP.mult, -1.0, OP.add)
+    tt(z("ad"), z("ta"), z("act"), OP.add)
+    ts(diff(U2), z("ad"), -1.0, OP.mult)
+    sign_b(0)
+    sign_a(0)
+    sign_b(1)
+    wrap_a(0)
 
     for k in range(ROUNDS):
-        old, new = ("om0", "om1") if k % 2 == 0 else ("om1", "om0")
+        new = "om1" if k % 2 == 0 else "om0"
         peer = T.cores[rank ^ STEP[k]]
         dl, la, last = "dl%d" % k, "la%d" % k, k == ROUNDS - 1
-        tt(("fr", 0, C), (("ew", 0, 2 * C), ("dst", 0, 24)), ("hrow", 0, C), OP.is_equal)
-        scan(("fs", 0, C), ("fr", 0, C), OP.add)
-        z = lambda n: (n, 0, 72)
-        f = ("mp", 0, 24)
-        ts(f, ends("fs"), "thp", OP.is_ge)
-        for j in (1, 2): tt(("mp", 24 * j, 24 * j + 24), ("dp", 24 * j, 24 * j + 24), f, OP.mult)
-        tt(z("sp"), z("mp"), z("p0"), OP.add)
-        cp(z("p16"), z("sp"))
-        move("A", ("pir", 1, F, 3), (("idr", 0, F), ("p16", 24, 48)))
-        move("A", ("pir", 2, 866, 3), (("idr", 0, F), ("p16", 48, 66)))
-        for j in range(3): tt(("mu", 24 * j, 24 * j + 24), ("du", 24 * j, 24 * j + 24), f, OP.mult)
-        tt(z("su"), z("mu"), z("u0"), OP.add)
-        cp(z("u16"), z("su"))
-        move("V", ("pir", 0, F, 3), (("idr", 0, F), ("p16", 0, 24)))
-        move("V", ("pir", 866, F, 3), (("idr", 0, F), ("p16", 66, 72)))
-        for q, j in (("V", 1), ("A", 0), ("A", 2)): move(q, (new, j, F, 3), (("pir", 0, F), ("u16", 24 * j, 24 * j + 24)))
-        scan(("sc", C, 2 * C), (new, 1, F, 3))
+        sign_a(1)
+        move("A", ("gr", 224, C), (("ew", 0, 2 * C), ("dst", 14, 24)))
+        wrap_a(1)
+        move("V", ("gr", 0, 224), (("ew", 0, 2 * C), ("dst", 0, 14)))
+        tt(z("hw"), ends("aw"), z("ink"), OP.max)
+        scan(("gs", 0, C), ("mk", 0, C), ("gr", 0, C), 0.0, OP.add)
+        halves(1)
+
+        def bit(i):
+            tt(("ca", 48 * i, 48 * i + 48, 2), ends("gs"), z("hw"), OP.is_equal)
+
+        def select(i, j):
+            scan(("co", 48 * i, 48 * j), ("cb", 48 * i, 48 * j), ("ca", 48 * i, 48 * j), 0.0, OP.add)
+
+        def cast(i, j):
+            cp(("l16", 24 * i, 24 * j), ("co", 48 * i + 1, 48 * j, 2))
+        for i in (P0, P1, U0): bit(i)
+        select(P0, U0)
+        for i in (U2, U1): bit(i)
+        cast(P0, U0)
+        select(U0, 5)
+
+        def row(b, j, lo=0, hi=C):
+            return (b, C * j + lo, C * j + hi) if k == 0 and b == "pir" else (b, 3 * lo + j, 3 * hi, 3)
+        move("A", row("pir", 1), (("idr", 0, F), chosen(P1)))
+        move("V", row("pir", 0), (("idr", 0, F), chosen(P0)))
+        cast(U0, 5)
+        move("A", row("pir", 2, 0, 192), (("t2", 0, F), chosen(P1, 0, 192)))
+        move("V", row("pir", 2, 192, C), (("t2", 0, F), chosen(P1, 192, C)))
+        source = "pir"
+        if k == 0:
+            source = "om0"
+            for q, j, lo, hi in (("V", 0, 0, C), ("A", 1, 0, C), ("V", 2, 0, 192), ("A", 2, 192, C)):
+                move(q, row(source, j, lo, hi), (("pir", 0, F), ("wl16", 24 * j + lo // 16, 24 * j + hi // 16)))
+        for q, j, i in (("V", 1, U1), ("A", 2, U2), ("A", 0, U0)): move(q, row(new, j), ((source, 0, F), chosen(i)))
+        wrap(("sc", C, 2 * C), row(new, 1))
         agents(("l12", 0, 24), ends("sc", 1))
-        scan(("sc", 0, C), (new, 0, F, 3))
-        ports((dl, 0, 24), ends("sc", 0))
-        scan(("sc", 2 * C, 3 * C), (new, 2, F, 3))
+        wrap(("sc", 2 * C, 3 * C), row(new, 2))
+        wrap(("sc", 0, C), row(new, 0))
         agents(("l12", 24, 48), ends("sc", 2))
+        ports((dl, 0, 24), ends("sc", 0))
         send(peer, T[la][:, 0:24], T[dl][:, 0:24], [(dl, 0, 24)], "al%d" % k)
         note("al%d" % k, len(topo.engines(core, peer)), [], [(la, 0, 24)])
         for i, (lo, hi) in enumerate(ZRUNS):
             for b in range(4): move("A", ("gz", C * b + lo, C * b + hi), (("xh", C * b, C * b + C), ("l12", lo // 16, hi // 16)))
         if not last:
-            for j, w in enumerate((W0, W1, W2)): wraps(w, ends("sc", j))
+            lin(("w", 24, 96), ends("sc", 0, 3), "inv", -1.0)
+            lin(value(U0), ends("sc", 0), "inv", -1.0)
         for i, (lo, hi) in enumerate(ZRUNS):
             for b in range(4): tt(("zt", 4 * lo + b, 4 * hi, 4), (("xh", C * b, C * b + C), ("l12", 24 + lo // 16, 24 + hi // 16)), ("gz", C * b + lo, C * b + hi), OP.add)
+            if i == 1 and not last: ports(z("wi"), ends("sc", 0))
             quant("zq", "zs", lo, hi, ("zt", 4 * lo, 4 * hi))
             for b in range(4): mm(4 * i + b, hi - lo, "wq", "wp", 128 * b, "zq", "zs", lo)
-        def look():
-            move("A", ("mr", 0, C), ((new, 0, F), (la, 0, 24)))
-
-        def places():
-            scan(("ms", 0, C), ("mr", 0, C))
-            agents(("ml", 0, 24), ends("ms"))
-        for n, (q, i, b) in enumerate((("A", 0, 0), ("A", 0, 1), ("V", 0, 2), ("A", 0, 3), ("V", 1, 0), ("A", 1, 1), ("V", 1, 2), ("A", 1, 3))):
-            if n == 1: look()
-            if n == 3: places()
-            lo, hi = ZRUNS[i]
-            scaled(q, ("hp", C * b + lo, C * b + hi), psum(4 * i + b, hi - lo), 0.03125)
+        move("A", ("mr", 0, C), ((new, 0, F), (la, 0, 24)))
+        wrap(("ms", 0, C), ("mr", 0, C))
+        if not last: tt(z("act"), W0, z("wi"), OP.is_gt)
+        agents(("ml", 0, 24), ends("ms"))
+        for i, (lo, hi) in enumerate(ZRUNS):
+            for q, b in zip(EVACUATE[i], range(4)): scaled(q, ("hp", C * b + lo, C * b + hi), psum(4 * i + b, hi - lo), 0.03125)
         hq, hs, lq, ls = "hq%d" % k, "hs%d" % k, "lq%d" % k, "ls%d" % k
         for i, (lo, hi) in enumerate(EXCHANGE[k]):
-            for q, b in (("V", 0), ("A", 1), ("V", 2), ("A", 3)):
+            for q, b in zip(PICK[k][i], range(4)):
                 move(q, ("hg", 4 * lo + b, 4 * hi, 4), (("hp", C * b, C * b + C), ("ml", lo // 16, hi // 16)))
+            if not last and i == 0: tt(z("td"), W0, z("c3"), OP.subtract)
+            if not last and i == 1:
+                tt(z("ad0"), W2, W1, OP.subtract)
+                principal()
             quant(hq, hs, lo, hi, ("hg", 4 * lo, 4 * hi))
             send(peer, T[lq][:, lo:hi].bitcast(dt.uint8), T[hq][:, lo:hi].bitcast(dt.uint8), [(hq, lo, hi)], "ah%d%d" % (k, i))
             send(peer, T[ls][:, lo:hi], T[hs][:, lo:hi], [(hs, lo, hi)], "ah%d%d" % (k, i))
             note("ah%d%d" % (k, i), 2 * len(topo.engines(core, peer)), [], [(lq, lo, hi), (ls, lo, hi)])
-        if k == 1: quant("vq", "vs", 0, 128, ("vt", 0, 512))
+        if k == 0:
+            for j in range(3): iota(("qtab", j, F, 3), [[1, C]], C * j, 0, True)
         if not last:
-            ready1(new, dl, 0, W0, W1, W2)
-            ready2()
+            ts(("x12", 0, 24), value(P1), 1.0, OP.add)
+            cp(("x12", 24, 48), value(P1))
+            flags()
+            for j in range(2): move("A", ("y12", C * j, C * j + C), ((new, 0, F), ("x12", 24 * j, 24 * j + 24)))
+            tt(z("ad"), z("ad0"), z("act"), OP.mult)
+            if k == 1: quant("vq", "vs", 0, 128, ("vt", 0, 512))
+            tt(z("u10"), W1, z("ad"), OP.add)
+            tt(("w", 0, 24), W2, z("ad"), OP.subtract)
+            deciding()
+            tt(diff(U0), z("u10"), W0, OP.subtract)
+            for j in range(2): wrap(("sy", C * j, C * j + C), ("y12", C * j, C * j + C))
+            lin(value(U2, 2), ends("sy", 0, 2), "inv", -1.0)
         else:
-            for j in range(3): ports(("fin", 24 * j, 24 * j + 24), ends("sc", j))
+            ports(("fin", 0, 72), ends("sc", 0, 3))
             move("A", ("owr", 0, F), (("qtab", 0, F), ("fin", 0, 72)))
             for j in range(8): dma("S", T.ow[j:j + 1, :], T.owr[16 * j:16 * j + 1, 0:F], [("owr", 0, F)], [])
         def unpack(i):
@@ -393,7 +416,6 @@ def rank_program(g, core, T, topo):
             for b in range(4):
                 x = ("xt", 4 * lo + b, 4 * hi, 4)
                 tt(x, psum(4 - 4 * (i % 2) + b, hi - lo), x, OP.add)
-            quantx(lo, hi)
 
         def store(bank, lo, hi):
             mm(bank, hi - lo, "vq", "vs", 0, "xq", "xs", lo)
@@ -404,21 +426,25 @@ def rank_program(g, core, T, topo):
         unpack(0)
         unpack(1)
         add(0)
+        quantx(*EXCHANGE[k][0])
         if not last:
             scores(0)
-            tt(("du", 24, 48), W0, ("u0", 24, 48), OP.subtract)
-            tt(("du", 48, 72), ("u12", 0, 24), ("u0", 48, 72), OP.subtract)
             halves(0)
             add(1)
+            tt(diff(U2, 2), ("w", 0, 48), value(U2, 2), OP.subtract)
+            quantx(*EXCHANGE[k][1])
             scores(1)
-            signs(0, "A")
-            signs(1)
-            halves(1)
+            sign_b(0)
+            sign_a(0)
+            sign_b(1)
+            wrap_a(0)
         else:
             unpack(2)
             add(1)
+            quantx(*EXCHANGE[k][1])
             store(0, 0, 256)
             add(2)
+            quantx(*EXCHANGE[k][2])
             store(1, 256, 384)
     for sem in ("V", "A", "P", "G", "left"): wait("G", sem, count[sem])
     for j in range(ndma[0]): wait("G", "d%d" % j, 16)

@@ -49,7 +49,7 @@ for _k in range(ROUNDS):
     for _n in ("h", "l"):
         SCRATCH["%sq%d" % (_n, _k)] = ("sbuf", [128, C], "float8_e4m3fn_x4")
         SCRATCH["%ss%d" % (_n, _k)] = ("sbuf", [128, C], "uint8")
-SEMAPHORES = ["V", "A", "P", "G", "left", "ae"] + ["al%d" % k for k in range(ROUNDS)] + ["ah%d%d" % (k, i) for k in range(ROUNDS) for i in range(len(EXCHANGE[k]))] + ["d%d" % i for i in range(40)]
+SEMAPHORES = ["V", "A", "P", "G", "left", "ae"] + ["al%d" % k for k in range(ROUNDS)] + ["ah%d%d" % (k, i) for k in range(ROUNDS) for i in range(3)] + ["d%d" % i for i in range(40)]
 
 
 def rank_program(g, core, T, topo):
@@ -162,7 +162,7 @@ def rank_program(g, core, T, topo):
         op("V", [d0, d1], [o], lambda e: e.tensor_tensor_scan(ap(o), ap(d0), ap(d1), first, OP.mult, f))
 
     def wrap(o, a):
-        scan(o, ("mn", 0, C), a, 1.0, OP.min)
+        scan(o, ("mn", 0, o[2] - o[1]), a, 1.0, OP.min)
 
     def quant(q, s, lo, hi, a):
         op("V", [a], [(q, lo, hi), (s, lo, hi)], lambda e: e.quantize_mx(T[q][:, lo:hi], T[s][:, lo:hi], ap(a)))
@@ -198,6 +198,7 @@ def rank_program(g, core, T, topo):
     dma("A", T.wlt[:, 0:72], T.wl[:, :], [], [("wlt", 0, 72)])
     dma("S", T.ut[:, 0:512], T.u[:, :], [], [("ut", 0, 512)])
     for i, (lo, hi) in enumerate(RUNS): dma("AS"[i], T.xt[:, 4 * lo:4 * hi], T.x[:, 4 * lo:4 * hi], [], [("xt", 4 * lo, 4 * hi)])
+    depend("S", [("xt", 0, 4 * C)], [])
     dma("S", T.wq[:, 0:512].bitcast(dt.uint8), T.wc[:, :], [], [("wq", 0, 512)])
     dma("S", T.wp[:, 0:512], T.ws[:, :], [], [("wp", 0, 512)])
     dma("S", T.vt[:, 0:512], T.v[:, :], [], [("vt", 0, 512)])
@@ -209,35 +210,29 @@ def rank_program(g, core, T, topo):
     iota(("c48", 0, 24), [[48, 24]], 0, 0, True)
     iota(("uoi", 0, 16), [[1, 2], [16, 8]], 0, 0, False)
     side = 0 if rank < (rank ^ STEP[0]) else 1
-    fill(("ones", 0, 516), 1.0)
-    ts(("p15i", 0, 1), ("pi32", 0, 1), 15, OP.bitwise_and)
     fill(("cb", 0, 240), 0.0)
+    ts(("p15i", 0, 1), ("pi32", 0, 1), 15, OP.bitwise_and)
+    fill(("ones", 0, 516), 1.0)
     cp(("p15", 0, 1), ("p15i", 0, 1))
     fill(diff(P0), 1.0)
     iota(("idr", 2, F, 3), [[3, C]], 3, 0, True)
     op("G", [("ones", 0, 516)], [("eb", 0, 516)], lambda e: e.affine_select(T.eb[:, 0:516], T.ones[:, 0:516], [[-1, 516]], OP.is_equal, 0.0, 3, 4))
     for j in range(2): iota(("t2", j, F, 3), [[3, C]], 3, 0, True)
+    j96 = ("jr", 0, 96)
     ts(("p16", 0, 1), ("p15", 0, 1), 1.0, OP.add)
     ts(("p3", 0, 1), ("p15", 0, 1), 3.0, OP.mult)
     ts(("last", 0, 1), ("p15", 0, 1), 15.0, OP.is_equal)
-    j96 = ("jr", 0, 96)
     ts(("e0", 0, 96), j96, "p15", OP.not_equal)
-    ts(("e1", 0, 96), j96, "p16", OP.is_equal, K, OP.mult)
     ts(("e2", 0, 96), j96, "p15", OP.is_equal, K, OP.mult)
+    cp(("uo", 0, 16), ("uoi", 0, 16))
+    ts(("e1", 0, 96), j96, "p16", OP.is_equal, K, OP.mult)
     ts(("e3", 0, 96), j96, "p16", OP.not_equal, SMALL, OP.max)
     ts(z("c3"), z("c48"), "p3", OP.add)
     ts(z("c31"), z("c48"), "p3", OP.add, 1.0, OP.add)
-    ts(value(P0), z("c48"), "p3", OP.add)
-    ts(value(U0), z("c48"), "p3", OP.add)
-    tt(("mk", 0, 96), ("e0", 0, 96), ("e1", 0, 96), OP.max)
-    tt(("mn", 0, 96), ("e2", 0, 96), ("e3", 0, 96), OP.max)
-    ts(("inv", 0, 1), ("last", 0, 1), 1.0 - 1.0 / SMALL, OP.mult, 1.0 / SMALL, OP.add)
-    ts(("inv3", 0, 1), ("last", 0, 1), (1.0 - 1.0 / SMALL) / 3.0, OP.mult, 1.0 / SMALL / 3.0, OP.add)
     ts(("thp", 0, 1), ("last", 0, 1), 1.0 - K, OP.mult, K, OP.add)
-    cp(("uo", 0, 16), ("uoi", 0, 16))
-    for lo in (96, 192):
-        for m in ("mk", "mn"): cp((m, lo, 2 * lo), (m, 0, lo))
-    for j, b in ((0, -1.875), (1, -1.0)): lin(("idr", j, F, 3), ("idr", 2, F, 3), 1.0, b)
+    ts(value(P0), z("c48"), "p3", OP.add)
+    tt(("mk", 0, 96), ("e0", 0, 96), ("e1", 0, 96), OP.max)
+    lin(("idr", 0, F, 3), ("idr", 2, F, 3), 1.0, -1.875)
 
     W0, W1, W2 = ("w", 24, 48), ("w", 48, 72), ("w", 72, 96)
 
@@ -246,70 +241,79 @@ def rank_program(g, core, T, topo):
         lin(z("a2m"), z("act"), 2.0, -1.0)
         lin(z("ink"), z("act"), -2.0 * K, "thp")
 
-    def principal():
-        tt(z("ta"), z("td"), z("act"), OP.mult)
-        tt(value(P1), z("ta"), z("c31"), OP.add)
-
-    def deciding():
-        tt(z("vta"), z("va"), value(P1), OP.add)
-        tt(diff(P1), z("a2m"), z("ta"), OP.subtract)
-        ts(z("dst"), z("vta"), 1.0 / 3.0, OP.mult)
-
     def quantx(lo, hi):
         quant("xq", "xs", lo, hi, ("xt", 4 * lo, 4 * hi))
 
+    state = {"runs": RUNS, "bank": 4}
+
     def scores(i):
-        lo, hi = RUNS[i]
-        mm(5 - 4 * i, hi - lo, "pq", "psc", 128, "xq", "xs", lo)
-        mm(4 - 4 * i, hi - lo, "pq", "psc", 0, "xq", "xs", lo)
+        lo, hi = state["runs"][i]
+        mm(state["bank"] + 2 * i + 1, hi - lo, "pq", "psc", 128, "xq", "xs", lo)
+        mm(state["bank"] + 2 * i, hi - lo, "pq", "psc", 0, "xq", "xs", lo)
 
     def sign_a(i):
-        lo, hi = RUNS[i]
-        ts(("ew", lo, hi), psum(4 - 4 * i, hi - lo), 0.0, OP.is_gt, 0.5, OP.subtract)
+        lo, hi = state["runs"][i]
+        ts(("ew", lo, hi), psum(state["bank"] + 2 * i, hi - lo), 0.0, OP.is_gt, 0.5, OP.subtract)
 
     def sign_b(i):
-        lo, hi = RUNS[i]
-        ac(("ew", C + lo, C + hi), psum(5 - 4 * i, hi - lo), AF.Sign)
+        lo, hi = state["runs"][i]
+        ac(("ew", C + lo, C + hi), psum(state["bank"] + 2 * i + 1, hi - lo), AF.Sign)
 
     def wrap_a(i):
-        lo, hi = RUNS[i]
+        lo, hi = state["runs"][i]
         scan(("aw", lo, hi), ("mk", lo, hi), ("ew", lo, hi), 0.0, OP.add)
 
     def halves(i):
-        lo, hi = RUNS[i]
+        lo, hi = state["runs"][i]
         for b in range(4): ac(("xh", C * b + lo, C * b + hi), ("xt", 4 * lo + b, 4 * hi, 4), scale=0.5)
 
     w0 = ("wlt", 0, 24)
     ts(z("act"), w0, float(C), OP.is_lt)
     ts(z("q3"), w0, 3.0, OP.mult)
-    cp(("wl16", 0, 72), ("wlt", 0, 72))
+    cp(("mk", 96, 192), ("mk", 0, 96))
+    tt(("mn", 0, 96), ("e2", 0, 96), ("e3", 0, 96), OP.max)
     tt(z("td"), z("q3"), z("c3"), OP.subtract)
-    quant("uq", "us", 0, 128, ("ut", 0, 512))
     flags()
-    principal()
+    quant("uq", "us", 0, 128, ("ut", 0, 512))
+    cp(("mk", 192, C), ("mk", 0, 192))
+    tt(z("ta"), z("td"), z("act"), OP.mult)
+    cp(("mn", 96, 192), ("mn", 0, 96))
     op("A", [("us", 0, 128), ("uo", 0, 16)], [("psc", 0, 256)], lambda e: e.activation(T.psc[:, 0:256], T.us[:, 0:128].indirect(T.uo[:, 0:16]), AF.Copy))
     op("V", [("uq", 0, 128), ("uo", 0, 16)], [("pq", 0, 256)], lambda e: e.tensor_copy(T.pq[:, 0:256].bitcast(dt.uint32), T.uq[:, 0:128].bitcast(dt.uint32).indirect(T.uo[:, 0:16])))
-    deciding()
-    for j in range(2): quant("em", "ems", 128 * j, 128 * j + 128, ("eb", 3 - 2 * side - j, 515 - 2 * side - j))
-    for lo, hi in RUNS: quantx(lo, hi)
+    tt(value(P1), z("ta"), z("c31"), OP.add)
+    quantx(*RUNS[0])
     scores(0)
-    scores(1)
+    lin(("idr", 1, F, 3), ("idr", 2, F, 3), 1.0, -1.0)
+    ac(("t2", 2, F, 3), ("idr", 0, F, 3))
+    tt(z("vta"), z("va"), value(P1), OP.add)
+    for j in range(2): quant("em", "ems", 128 * j, 128 * j + 128, ("eb", 3 - 2 * side - j, 515 - 2 * side - j))
+    ts(z("dst"), z("vta"), 1.0 / 3.0, OP.mult)
     mate = T.cores[rank ^ STEP[0]]
     send(mate, T.el[:, 0:256].bitcast(dt.uint8), T.em[:, 0:256].bitcast(dt.uint8), [("em", 0, 256)], "ae")
     send(mate, T.els[:, 0:256], T.ems[:, 0:256], [("ems", 0, 256)], "ae")
     note("ae", 2 * len(topo.engines(core, mate)), [], [("el", 0, 256), ("els", 0, 256)])
-    ac(("t2", 2, F, 3), ("idr", 0, F, 3))
-    halves(0)
-    ts(diff(U0), z("act"), 1.0, OP.add)
-    cp(value(U1), value(P1))
-    ts(value(U2), value(P1), 1.0, OP.add)
-    ts(diff(U1), z("ta"), -1.0, OP.mult, -1.0, OP.add)
-    tt(z("ad"), z("ta"), z("act"), OP.add)
-    ts(diff(U2), z("ad"), -1.0, OP.mult)
+    quantx(*RUNS[1])
+    scores(1)
     sign_b(0)
     sign_a(0)
     sign_b(1)
+    tt(diff(P1), z("a2m"), z("ta"), OP.subtract)
+    tt(z("ad"), z("ta"), z("act"), OP.add)
+    ts(value(U0), z("c48"), "p3", OP.add)
+    ts(diff(U0), z("act"), 1.0, OP.add)
     wrap_a(0)
+    cp(value(U1), value(P1))
+    ts(value(U2), value(P1), 1.0, OP.add)
+
+    def rest():
+        ts(diff(U1), z("ta"), -1.0, OP.mult, -1.0, OP.add)
+        ts(diff(U2), z("ad"), -1.0, OP.mult)
+        cp(("mn", 192, C), ("mn", 0, 192))
+        cp(("wl16", 0, 72), ("wlt", 0, 72))
+
+    def rest2():
+        ts(("inv", 0, 1), ("last", 0, 1), 1.0 - 1.0 / SMALL, OP.mult, 1.0 / SMALL, OP.add)
+        ts(("inv3", 0, 1), ("last", 0, 1), (1.0 - 1.0 / SMALL) / 3.0, OP.mult, 1.0 / SMALL / 3.0, OP.add)
 
     for k in range(ROUNDS):
         new = "om1" if k % 2 == 0 else "om0"
@@ -320,7 +324,11 @@ def rank_program(g, core, T, topo):
         wrap_a(1)
         move("V", ("gr", 0, 224), (("ew", 0, 2 * C), ("dst", 0, 14)))
         tt(z("hw"), ends("aw"), z("ink"), OP.max)
+        if k == 0: rest2()
         scan(("gs", 0, C), ("mk", 0, C), ("gr", 0, C), 0.0, OP.add)
+        if k == 0:
+            rest()
+            halves(0)
         halves(1)
 
         def bit(i):
@@ -331,17 +339,16 @@ def rank_program(g, core, T, topo):
 
         def cast(i, j):
             cp(("l16", 24 * i, 24 * j), ("co", 48 * i + 1, 48 * j, 2))
-        for i in (P0, P1, U0): bit(i)
+        for i in range(5): bit(i)
         select(P0, U0)
-        for i in (U2, U1): bit(i)
-        cast(P0, U0)
         select(U0, 5)
+        cast(P0, U0)
+        cast(U0, 5)
 
         def row(b, j, lo=0, hi=C):
             return (b, C * j + lo, C * j + hi) if k == 0 and b == "pir" else (b, 3 * lo + j, 3 * hi, 3)
         move("A", row("pir", 1), (("idr", 0, F), chosen(P1)))
         move("V", row("pir", 0), (("idr", 0, F), chosen(P0)))
-        cast(U0, 5)
         move("A", row("pir", 2, 0, 192), (("t2", 0, F), chosen(P1, 0, 192)))
         move("V", row("pir", 2, 192, C), (("t2", 0, F), chosen(P1, 192, C)))
         source = "pir"
@@ -349,39 +356,89 @@ def rank_program(g, core, T, topo):
             source = "om0"
             for q, j, lo, hi in (("V", 0, 0, C), ("A", 1, 0, C), ("V", 2, 0, 192), ("A", 2, 192, C)):
                 move(q, row(source, j, lo, hi), (("pir", 0, F), ("wl16", 24 * j + lo // 16, 24 * j + hi // 16)))
-        for q, j, i in (("V", 1, U1), ("A", 2, U2), ("A", 0, U0)): move(q, row(new, j), ((source, 0, F), chosen(i)))
-        wrap(("sc", C, 2 * C), row(new, 1))
-        agents(("l12", 0, 24), ends("sc", 1))
-        wrap(("sc", 2 * C, 3 * C), row(new, 2))
-        wrap(("sc", 0, C), row(new, 0))
-        agents(("l12", 24, 48), ends("sc", 2))
+        def rewire(q, j, lo=0, hi=C):
+            move(q, row(new, j, lo, hi), ((source, 0, F), chosen((U0, U1, U2)[j], lo, hi)))
+
+        def wrapped(j, lo=0, hi=C):
+            wrap(("sc", C * j + lo, C * j + hi), row(new, j, lo, hi))
+
+        def listed(j, lo=0, hi=C):
+            agents(("l12", 24 * (j - 1) + lo // 16, 24 * (j - 1) + hi // 16), ("sc", C * j + lo + 15, C * j + hi, 16))
+        cut = ZRUNS[0][1]
+        rewire("V", 1, 0, cut)
+        rewire("A", 2)
+        rewire("V", 1, cut, C)
+        rewire("A", 0)
+        wrapped(1, 0, cut)
+        wrapped(2)
+        listed(1, 0, cut)
+        wrapped(1, cut, C)
+        listed(2)
+        wrapped(0)
+        listed(1, cut, C)
         ports((dl, 0, 24), ends("sc", 0))
         send(peer, T[la][:, 0:24], T[dl][:, 0:24], [(dl, 0, 24)], "al%d" % k)
         note("al%d" % k, len(topo.engines(core, peer)), [], [(la, 0, 24)])
+
+        def level(i):
+            if last: return
+            if i == 0:
+                ports(z("wi"), ends("sc", 0))
+                tt(z("td"), W0, z("c3"), OP.subtract)
+                tt(z("ad0"), W2, W1, OP.subtract)
+            if i == 1: tt(z("act"), W0, z("wi"), OP.is_gt)
+            if i == 2:
+                tt(z("ta"), z("td"), z("act"), OP.mult)
+                tt(z("ad"), z("ad0"), z("act"), OP.mult)
+                flags()
+            if i == 3:
+                tt(value(P1), z("ta"), z("c31"), OP.add)
+                tt(z("u10"), W1, z("ad"), OP.add)
+                tt(("w", 0, 24), W2, z("ad"), OP.subtract)
+                tt(diff(P1), z("a2m"), z("ta"), OP.subtract)
+            if i == 4:
+                ts(("x12", 0, 24), value(P1), 1.0, OP.add)
+                cp(("x12", 24, 48), value(P1))
+                tt(z("vta"), z("va"), value(P1), OP.add)
+                tt(diff(U0), z("u10"), W0, OP.subtract)
         for i, (lo, hi) in enumerate(ZRUNS):
             for b in range(4): move("A", ("gz", C * b + lo, C * b + hi), (("xh", C * b, C * b + C), ("l12", lo // 16, hi // 16)))
         if not last:
             lin(("w", 24, 96), ends("sc", 0, 3), "inv", -1.0)
             lin(value(U0), ends("sc", 0), "inv", -1.0)
-        for i, (lo, hi) in enumerate(ZRUNS):
-            for b in range(4): tt(("zt", 4 * lo + b, 4 * hi, 4), (("xh", C * b, C * b + C), ("l12", 24 + lo // 16, 24 + hi // 16)), ("gz", C * b + lo, C * b + hi), OP.add)
-            if i == 1 and not last: ports(z("wi"), ends("sc", 0))
+
+        def layer(i):
+            lo, hi = ZRUNS[i]
             quant("zq", "zs", lo, hi, ("zt", 4 * lo, 4 * hi))
-            for b in range(4): mm(4 * i + b, hi - lo, "wq", "wp", 128 * b, "zq", "zs", lo)
+            for b in range(4): mm(4 * (i % 2) + b, hi - lo, "wq", "wp", 128 * b, "zq", "zs", lo)
+
+        def evacuate(i):
+            lo, hi = ZRUNS[i]
+            for q, b in zip(EVACUATE[i], range(4)): scaled(q, ("hp", C * b + lo, C * b + hi), psum(4 * (i % 2) + b, hi - lo), 0.03125)
+        for i, (lo, hi) in enumerate(ZRUNS):
+            for b in range(4):
+                tt(("zt", 4 * lo + b, 4 * hi, 4), (("xh", C * b, C * b + C), ("l12", 24 + lo // 16, 24 + hi // 16)), ("gz", C * b + lo, C * b + hi), OP.add)
+                if i > 0 and b == 0: layer(i - 1)
+        level(0)
+        for i in range(len(ZRUNS) - 2): evacuate(i)
+        layer(len(ZRUNS) - 1)
         move("A", ("mr", 0, C), ((new, 0, F), (la, 0, 24)))
         wrap(("ms", 0, C), ("mr", 0, C))
-        if not last: tt(z("act"), W0, z("wi"), OP.is_gt)
+        level(1)
+        evacuate(len(ZRUNS) - 2)
         agents(("ml", 0, 24), ends("ms"))
-        for i, (lo, hi) in enumerate(ZRUNS):
-            for q, b in zip(EVACUATE[i], range(4)): scaled(q, ("hp", C * b + lo, C * b + hi), psum(4 * i + b, hi - lo), 0.03125)
+        level(2)
+        evacuate(len(ZRUNS) - 1)
         hq, hs, lq, ls = "hq%d" % k, "hs%d" % k, "lq%d" % k, "ls%d" % k
+        def pick(i, b):
+            lo, hi = EXCHANGE[k][i]
+            move(PICK[k][i][b], ("hg", 4 * lo + b, 4 * hi, 4), (("hp", C * b, C * b + C), ("ml", lo // 16, hi // 16)))
         for i, (lo, hi) in enumerate(EXCHANGE[k]):
-            for q, b in zip(PICK[k][i], range(4)):
-                move(q, ("hg", 4 * lo + b, 4 * hi, 4), (("hp", C * b, C * b + C), ("ml", lo // 16, hi // 16)))
-            if not last and i == 0: tt(z("td"), W0, z("c3"), OP.subtract)
-            if not last and i == 1:
-                tt(z("ad0"), W2, W1, OP.subtract)
-                principal()
+            for b in range(4):
+                if not (last and i > 0 and b == 3): pick(i, b)
+            if i < 2: level(3 + i)
+            if last and hi < C: pick(i + 1, 3)
+            if last and hi == C: ports(("fin", 0, 72), ends("sc", 0, 3))
             quant(hq, hs, lo, hi, ("hg", 4 * lo, 4 * hi))
             send(peer, T[lq][:, lo:hi].bitcast(dt.uint8), T[hq][:, lo:hi].bitcast(dt.uint8), [(hq, lo, hi)], "ah%d%d" % (k, i))
             send(peer, T[ls][:, lo:hi], T[hs][:, lo:hi], [(hs, lo, hi)], "ah%d%d" % (k, i))
@@ -389,20 +446,11 @@ def rank_program(g, core, T, topo):
         if k == 0:
             for j in range(3): iota(("qtab", j, F, 3), [[1, C]], C * j, 0, True)
         if not last:
-            ts(("x12", 0, 24), value(P1), 1.0, OP.add)
-            cp(("x12", 24, 48), value(P1))
-            flags()
             for j in range(2): move("A", ("y12", C * j, C * j + C), ((new, 0, F), ("x12", 24 * j, 24 * j + 24)))
-            tt(z("ad"), z("ad0"), z("act"), OP.mult)
+            ts(z("dst"), z("vta"), 1.0 / 3.0, OP.mult)
             if k == 1: quant("vq", "vs", 0, 128, ("vt", 0, 512))
-            tt(z("u10"), W1, z("ad"), OP.add)
-            tt(("w", 0, 24), W2, z("ad"), OP.subtract)
-            deciding()
-            tt(diff(U0), z("u10"), W0, OP.subtract)
-            for j in range(2): wrap(("sy", C * j, C * j + C), ("y12", C * j, C * j + C))
-            lin(value(U2, 2), ends("sy", 0, 2), "inv", -1.0)
+            wrap(("sy", 0, C), ("y12", 0, C))
         else:
-            ports(("fin", 0, 72), ends("sc", 0, 3))
             move("A", ("owr", 0, F), (("qtab", 0, F), ("fin", 0, 72)))
             for j in range(8): dma("S", T.ow[j:j + 1, :], T.owr[16 * j:16 * j + 1, 0:F], [("owr", 0, F)], [])
         def unpack(i):
@@ -423,28 +471,32 @@ def rank_program(g, core, T, topo):
             for j in range(4): dma("A" if j % 2 else "S", T.osc[4 * j:4 * j + 4, lo:hi], T.xs[32 * j:32 * j + 4, lo:hi], [("xs", lo, hi)], [])
             ac(("yt", lo, hi), psum(bank, hi - lo))
             dma("A", T.y[:, lo:hi], T.yt[:, lo:hi], [("yt", lo, hi)], [])
+        n = len(EXCHANGE[k])
+        state["runs"], state["bank"] = [(0, EXCHANGE[k][-1][0]), EXCHANGE[k][-1]], 4 - 4 * (n % 2)
         unpack(0)
         unpack(1)
-        add(0)
-        quantx(*EXCHANGE[k][0])
+        for i in range(n - 1):
+            add(i)
+            if i + 2 < n: unpack(i + 2)
+        if not last:
+            wrap(("sy", C, 2 * C), ("y12", C, 2 * C))
+            lin(value(U2, 2), ends("sy", 0, 2), "inv", -1.0)
+        quantx(*state["runs"][0])
         if not last:
             scores(0)
             halves(0)
-            add(1)
+            add(n - 1)
             tt(diff(U2, 2), ("w", 0, 48), value(U2, 2), OP.subtract)
-            quantx(*EXCHANGE[k][1])
+            quantx(*state["runs"][1])
             scores(1)
             sign_b(0)
             sign_a(0)
             sign_b(1)
             wrap_a(0)
         else:
-            unpack(2)
-            add(1)
-            quantx(*EXCHANGE[k][1])
-            store(0, 0, 256)
-            add(2)
-            quantx(*EXCHANGE[k][2])
-            store(1, 256, 384)
+            store(state["bank"], *state["runs"][0])
+            add(n - 1)
+            quantx(*state["runs"][1])
+            store(state["bank"] + 1, *state["runs"][1])
     for sem in ("V", "A", "P", "G", "left"): wait("G", sem, count[sem])
     for j in range(ndma[0]): wait("G", "d%d" % j, 16)

from concourse.mybir import dt, AluOpType, ActivationFunctionType as AF

OP = AluOpType
C = 384
F = 3 * C
K = 4194304.0
SMALL = 1.0 / 2048
ROUNDS = 3
STEP = [1, 2, 3]
RUNS = [(0, 192), (192, 384)]
EXCHANGE = [RUNS, RUNS, [(0, 128), (128, 256), (256, 384)]]
ZRUNS = [(0, 256), (256, 384)]
EVACUATE = ["AAVA", "VVVV"]
PICK = [["AAVV", "AAAV"], ["AAVV", "AAAV"], ["AAVV", "AAVV", "AAAV"]]
P0, P1, U0, U2, U1 = range(5)

SCRATCH = {
    "xt": ("sbuf", [128, 4 * C], "bfloat16"), "xh": ("sbuf", [128, 4 * C], "bfloat16"), "gz": ("sbuf", [128, 4 * C], "bfloat16"),
    "zt": ("sbuf", [128, 4 * C], "bfloat16"), "hp": ("sbuf", [128, 4 * C], "bfloat16"), "hg": ("sbuf", [128, 4 * C], "bfloat16"),
    "ut": ("sbuf", [128, 512], "bfloat16"), "vt": ("sbuf", [128, 512], "bfloat16"),
    "ones": ("sbuf", [128, 516], "bfloat16"), "eb": ("sbuf", [128, 516], "bfloat16"),
    "uq": ("sbuf", [128, 128], "float8_e4m3fn_x4"), "us": ("sbuf", [128, 128], "uint8"),
    "pq": ("sbuf", [128, 256], "float8_e4m3fn_x4"), "psc": ("sbuf", [128, 256], "uint8"),
    "vq": ("sbuf", [128, 128], "float8_e4m3fn_x4"), "vs": ("sbuf", [128, 128], "uint8"),
    "em": ("sbuf", [128, 256], "float8_e4m3fn_x4"), "ems": ("sbuf", [128, 256], "uint8"), "el": ("sbuf", [128, 256], "float8_e4m3fn_x4"), "els": ("sbuf", [128, 256], "uint8"),
    "wq": ("sbuf", [128, 512], "float8_e4m3fn_x4"), "wp": ("sbuf", [128, 512], "uint8"),
    "xq": ("sbuf", [128, C], "float8_e4m3fn_x4"), "xs": ("sbuf", [128, C], "uint8"),
    "zq": ("sbuf", [128, C], "float8_e4m3fn_x4"), "zs": ("sbuf", [128, C], "uint8"),
    "wlt": ("sbuf", [128, 72], "int32"), "wl16": ("sbuf", [128, 72], "uint16"), "pi32": ("sbuf", [128, 1], "int32"), "p15i": ("sbuf", [128, 1], "int32"),
    "uoi": ("sbuf", [128, 16], "int32"), "uo": ("sbuf", [128, 16], "uint16"),
    "mk": ("sbuf", [128, C], "bfloat16"), "mn": ("sbuf", [128, C], "bfloat16"),
    "idr": ("sbuf", [128, F], "float32"), "t2": ("sbuf", [128, F], "float32"), "qtab": ("sbuf", [128, F], "float32"),
    "pir": ("sbuf", [128, F], "float32"), "om0": ("sbuf", [128, F], "float32"), "om1": ("sbuf", [128, F], "float32"),
    "ew": ("sbuf", [128, 2 * C], "bfloat16"), "gr": ("sbuf", [128, C], "bfloat16"), "gs": ("sbuf", [128, C], "bfloat16"), "aw": ("sbuf", [128, C], "bfloat16"),
    "cb": ("sbuf", [128, 240], "float32"), "ca": ("sbuf", [128, 240], "float32"), "co": ("sbuf", [128, 240], "float32"), "l16": ("sbuf", [128, 120], "uint16"),
    "sc": ("sbuf", [128, F], "float32"), "y12": ("sbuf", [128, 2 * C], "float16"), "sy": ("sbuf", [128, 2 * C], "float16"),
    "mr": ("sbuf", [128, C], "float16"), "ms": ("sbuf", [128, C], "float16"), "ml": ("sbuf", [128, 24], "uint16"),
    "l12": ("sbuf", [128, 48], "uint16"), "x12": ("sbuf", [128, 48], "uint16"), "w": ("sbuf", [128, 96], "float32"),
    "wi": ("sbuf", [128, 24], "int32"), "dst": ("sbuf", [128, 24], "uint16"),
    "fin": ("sbuf", [128, 72], "uint16"), "owr": ("sbuf", [128, F], "float32"), "yt": ("sbuf", [128, C], "float32"),
    "ps": ("psum", [128, 4096], "float32"),
}
for _n in ("p15", "p16", "p3", "last", "inv", "inv3", "thp"): SCRATCH[_n] = ("sbuf", [128, 1], "float32")
for _n in ("c48", "c3", "c31", "act", "td", "ta", "ad0", "ad", "a2m", "va", "vta", "u10", "hw", "ink", "q3"): SCRATCH[_n] = ("sbuf", [128, 24], "float32")
for _n in ("jr", "e0", "e1", "e2", "e3"): SCRATCH[_n] = ("sbuf", [128, 96], "bfloat16")
for _k in range(ROUNDS):
    SCRATCH["dl%d" % _k] = ("sbuf", [128, 24], "uint16")
    SCRATCH["la%d" % _k] = ("sbuf", [128, 24], "uint16")
    for _n in ("h", "l"):
        SCRATCH["%sq%d" % (_n, _k)] = ("sbuf", [128, C], "float8_e4m3fn_x4")
        SCRATCH["%ss%d" % (_n, _k)] = ("sbuf", [128, C], "uint8")
SEMAPHORES = ["V", "A", "P", "G", "left", "ae"] + ["al%d" % k for k in range(ROUNDS)] + ["ah%d%d" % (k, i) for k in range(ROUNDS) for i in range(3)] + ["d%d" % i for i in range(40)]


def rank_program(g, core, T, topo):
    rank = T.rank_of(core)
    if rank is None:
        return
    QUEUE = {"V": g.vector, "A": g.scalar, "P": g.tensor, "G": g, "S": g.sync}
    count = {}
    seen = {}
    book = {}

    def wait(q, sem, val):
        if seen.get((q, sem), 0) < val:
            QUEUE[q].wait_ge(T.sem[sem], val)
            seen[(q, sem)] = val

    def region(r):
        if len(r) == 3: return r[0], r[1], r[2], 1, 0
        return r[0], r[1], r[2], r[3], r[1] % r[3]

    def meets(a, b):
        if a[0] >= b[1] or b[0] >= a[1]: return False
        return not (a[2] == b[2] and a[3] != b[3])

    def note(sem, val, reads, writes):
        for r in reads:
            n, lo, hi, st, ph = region(r)
            book.setdefault(n, []).append((lo, hi, st, ph, sem, val, False))
        for r in writes:
            n, lo, hi, st, ph = region(r)
            l = [e for e in book.get(n, []) if not (lo <= e[0] and e[1] <= hi and (st == 1 or (st, ph) == (e[2], e[3])))]
            book[n] = l + [(lo, hi, st, ph, sem, val, True)]

    def depend(q, reads, writes):
        need = {}
        for rs, w in ((reads, False), (writes, True)):
            for r in rs:
                n, lo, hi, st, ph = region(r)
                for e in book.get(n, []):
                    if (w or e[6]) and meets((lo, hi, st, ph), e): need[e[4]] = max(need.get(e[4], 0), e[5])
        for sem in sorted(need): wait(q, sem, need[sem])

    def op(q, reads, writes, call):
        depend(q, reads, writes)
        count[q] = count.get(q, 0) + 1
        call(QUEUE[q]).then_inc(T.sem[q], 1)
        note(q, count[q], reads, writes)

    ndma = [0]

    def dma(q, out, in_, reads, writes):
        depend(q, reads, writes)
        sem = "d%d" % ndma[0]
        ndma[0] += 1
        count[sem] = 16
        QUEUE[q].dma_start(out, in_).then_inc(T.sem[sem], 16)
        note(sem, 16, reads, writes)

    def send(dst, out, in_, reads, sem):
        depend("G", reads, [])
        rid, pid, _ = topo.addr(dst)
        m = topo.mask(core, dst)
        count["left"] = count.get("left", 0) + len(topo.engines(core, dst))
        g.remote_dma(out, in_, T.sem[sem], T.sem.left, pid, rid, m)

    def ap(r):
        return T[r[0]][:, r[1]:r[2]] if len(r) == 3 else T[r[0]][:, r[1]:r[2]:r[3]]

    def apx(r):
        return (ap(r[0]).indirect(ap(r[1])), [r[0], r[1]]) if not isinstance(r[0], str) else (ap(r), [r])

    def column(s, rd):
        if not isinstance(s, str): return s
        rd.append((s, 0, 1))
        return T[s][:, 0:1]

    def tt(o, a, b, f):
        x, rd = apx(a)
        op("V", rd + [b], [o], lambda e: e.tensor_tensor(ap(o), x, ap(b), f))

    def ts(o, a, s1, f1, s2=None, f2=None):
        x, rd = apx(a)
        s1, s2 = column(s1, rd), column(s2, rd)
        if f2 is None: op("V", rd, [o], lambda e: e.tensor_scalar(ap(o), x, s1, None, f1))
        else: op("V", rd, [o], lambda e: e.tensor_scalar(ap(o), x, s1, s2, f1, f2))

    def cp(o, a):
        x, rd = apx(a)
        op("V", rd, [o], lambda e: e.tensor_copy(ap(o), x))

    def ac(o, a, f=AF.Copy, scale=1.0, bias=0.0):
        x, rd = apx(a)
        arg = {n: column(s, rd) for n, s, plain in (("bias", bias, 0.0), ("scale", scale, 1.0)) if s != plain}
        op("A", rd, [o], lambda e: e.activation(ap(o), x, f, **arg))

    def lin(o, a, scale, bias):
        ac(o, a, AF.Identity, scale=scale, bias=bias)

    def fill(o, v):
        op("V", [], [o], lambda e: e.memset(ap(o), v))

    def move(q, o, a):
        (cp if q == "V" else ac)(o, a)

    def scaled(q, o, a, s):
        if q == "V": ts(o, a, s, OP.mult)
        else: ac(o, a, scale=s)

    def scan(o, d0, d1, first, f):
        op("V", [d0, d1], [o], lambda e: e.tensor_tensor_scan(ap(o), ap(d0), ap(d1), first, OP.mult, f))

    def wrap(o, a):
        scan(o, ("mn", 0, o[2] - o[1]), a, 1.0, OP.min)

    def quant(q, s, lo, hi, a):
        op("V", [a], [(q, lo, hi), (s, lo, hi)], lambda e: e.quantize_mx(T[q][:, lo:hi], T[s][:, lo:hi], ap(a)))

    def mm(bank, n, w, ws, wlo, x, xs, lo):
        op("P", [(w, wlo, wlo + 128), (ws, wlo, wlo + 128), (x, lo, lo + n), (xs, lo, lo + n)], [("ps", 512 * bank, 512 * bank + 512)],
           lambda e: e.matmul_mx(T.ps[:, 512 * bank:512 * bank + n], T[w][:, wlo:wlo + 128], T[ws][:, wlo:wlo + 128], T[x][:, lo:lo + n], T[xs][:, lo:lo + n], True, True))

    def psum(bank, n):
        return ("ps", 512 * bank, 512 * bank + n)

    def z(n):
        return (n, 0, 24)

    def ends(b, i=0, n=1):
        return (b, C * i + 15, C * (i + n), 16)

    def ports(o, s):
        ts(o, s, "inv", OP.mult, -1.0, OP.add)

    def agents(o, s):
        ts(o, s, "inv3", OP.mult, -2.0 / 3.0, OP.add)

    def value(i, n=1):
        return ("ca", 48 * i + 1, 48 * (i + n), 2)

    def diff(i, n=1):
        return ("cb", 48 * i + 1, 48 * (i + n), 2)

    def chosen(i, lo=0, hi=C):
        return ("l16", 24 * i + lo // 16, 24 * i + hi // 16)

    dma("A", T.wlt[:, 0:72], T.wl[:, :], [], [("wlt", 0, 72)])
    dma("S", T.ut[:, 0:512], T.u[:, :], [], [("ut", 0, 512)])
    for i, (lo, hi) in enumerate(RUNS): dma("AS"[i], T.xt[:, 4 * lo:4 * hi], T.x[:, 4 * lo:4 * hi], [], [("xt", 4 * lo, 4 * hi)])
    depend("S", [("xt", 0, 4 * C)], [])
    dma("S", T.wq[:, 0:512].bitcast(dt.uint8), T.wc[:, :], [], [("wq", 0, 512)])
    dma("S", T.wp[:, 0:512], T.ws[:, :], [], [("wp", 0, 512)])
    dma("S", T.vt[:, 0:512], T.v[:, :], [], [("vt", 0, 512)])

    def iota(r, pattern, base, mult, flag):
        op("G", [], [r], lambda e: e.iota(ap(r), pattern, base, mult, allow_small_or_imprecise_dtypes=True) if flag else e.iota(ap(r), pattern, base, mult))
    iota(("pi32", 0, 1), [[0, 1]], 0, 1, False)
    iota(("jr", 0, 96), [[0, 6], [1, 16]], 0, 0, True)
    iota(("c48", 0, 24), [[48, 24]], 0, 0, True)
    iota(("uoi", 0, 16), [[1, 2], [16, 8]], 0, 0, False)
    side = 0 if rank < (rank ^ STEP[0]) else 1
    fill(("cb", 0, 240), 0.0)
    ts(("p15i", 0, 1), ("pi32", 0, 1), 15, OP.bitwise_and)
    fill(("ones", 0, 516), 1.0)
    cp(("p15", 0, 1), ("p15i", 0, 1))
    fill(diff(P0), 1.0)
    iota(("idr", 2, F, 3), [[3, C]], 3, 0, True)
    op("G", [("ones", 0, 516)], [("eb", 0, 516)], lambda e: e.affine_select(T.eb[:, 0:516], T.ones[:, 0:516], [[-1, 516]], OP.is_equal, 0.0, 3, 4))
    for j in range(2): iota(("t2", j, F, 3), [[3, C]], 3, 0, True)
    j96 = ("jr", 0, 96)
    ts(("p16", 0, 1), ("p15", 0, 1), 1.0, OP.add)
    ts(("p3", 0, 1), ("p15", 0, 1), 3.0, OP.mult)
    ts(("last", 0, 1), ("p15", 0, 1), 15.0, OP.is_equal)
    ts(("e0", 0, 96), j96, "p15", OP.not_equal)
    ts(("e2", 0, 96), j96, "p15", OP.is_equal, K, OP.mult)
    cp(("uo", 0, 16), ("uoi", 0, 16))
    ts(("e1", 0, 96), j96, "p16", OP.is_equal, K, OP.mult)
    ts(("e3", 0, 96), j96, "p16", OP.not_equal, SMALL, OP.max)
    ts(z("c3"), z("c48"), "p3", OP.add)
    ts(z("c31"), z("c48"), "p3", OP.add, 1.0, OP.add)
    ts(("thp", 0, 1), ("last", 0, 1), 1.0 - K, OP.mult, K, OP.add)
    ts(value(P0), z("c48"), "p3", OP.add)
    tt(("mk", 0, 96), ("e0", 0, 96), ("e1", 0, 96), OP.max)
    lin(("idr", 0, F, 3), ("idr", 2, F, 3), 1.0, -1.875)

    W0, W1, W2 = ("w", 24, 48), ("w", 48, 72), ("w", 72, 96)

    def flags():
        lin(z("va"), z("act"), -1152.0, 1151.0)
        lin(z("a2m"), z("act"), 2.0, -1.0)
        lin(z("ink"), z("act"), -2.0 * K, "thp")

    def quantx(lo, hi):
        quant("xq", "xs", lo, hi, ("xt", 4 * lo, 4 * hi))

    state = {"runs": RUNS, "bank": 4}

    def scores(i):
        lo, hi = state["runs"][i]
        mm(state["bank"] + 2 * i + 1, hi - lo, "pq", "psc", 128, "xq", "xs", lo)
        mm(state["bank"] + 2 * i, hi - lo, "pq", "psc", 0, "xq", "xs", lo)

    def sign_a(i):
        lo, hi = state["runs"][i]
        ts(("ew", lo, hi), psum(state["bank"] + 2 * i, hi - lo), 0.0, OP.is_gt, 0.5, OP.subtract)

    def sign_b(i):
        lo, hi = state["runs"][i]
        ac(("ew", C + lo, C + hi), psum(state["bank"] + 2 * i + 1, hi - lo), AF.Sign)

    def wrap_a(i):
        lo, hi = state["runs"][i]
        scan(("aw", lo, hi), ("mk", lo, hi), ("ew", lo, hi), 0.0, OP.add)

    def halves(i):
        lo, hi = state["runs"][i]
        for b in range(4): ac(("xh", C * b + lo, C * b + hi), ("xt", 4 * lo + b, 4 * hi, 4), scale=0.5)

    w0 = ("wlt", 0, 24)
    ts(z("act"), w0, float(C), OP.is_lt)
    ts(z("q3"), w0, 3.0, OP.mult)
    cp(("mk", 96, 192), ("mk", 0, 96))
    tt(("mn", 0, 96), ("e2", 0, 96), ("e3", 0, 96), OP.max)
    tt(z("td"), z("q3"), z("c3"), OP.subtract)
    flags()
    quant("uq", "us", 0, 128, ("ut", 0, 512))
    cp(("mk", 192, C), ("mk", 0, 192))
    tt(z("ta"), z("td"), z("act"), OP.mult)
    cp(("mn", 96, 192), ("mn", 0, 96))
    op("A", [("us", 0, 128), ("uo", 0, 16)], [("psc", 0, 256)], lambda e: e.activation(T.psc[:, 0:256], T.us[:, 0:128].indirect(T.uo[:, 0:16]), AF.Copy))
    op("V", [("uq", 0, 128), ("uo", 0, 16)], [("pq", 0, 256)], lambda e: e.tensor_copy(T.pq[:, 0:256].bitcast(dt.uint32), T.uq[:, 0:128].bitcast(dt.uint32).indirect(T.uo[:, 0:16])))
    tt(value(P1), z("ta"), z("c31"), OP.add)
    quantx(*RUNS[0])
    scores(0)
    lin(("idr", 1, F, 3), ("idr", 2, F, 3), 1.0, -1.0)
    ac(("t2", 2, F, 3), ("idr", 0, F, 3))
    tt(z("vta"), z("va"), value(P1), OP.add)
    for j in range(2): quant("em", "ems", 128 * j, 128 * j + 128, ("eb", 3 - 2 * side - j, 515 - 2 * side - j))
    ts(z("dst"), z("vta"), 1.0 / 3.0, OP.mult)
    mate = T.cores[rank ^ STEP[0]]
    send(mate, T.el[:, 0:256].bitcast(dt.uint8), T.em[:, 0:256].bitcast(dt.uint8), [("em", 0, 256)], "ae")
    send(mate, T.els[:, 0:256], T.ems[:, 0:256], [("ems", 0, 256)], "ae")
    note("ae", 2 * len(topo.engines(core, mate)), [], [("el", 0, 256), ("els", 0, 256)])
    quantx(*RUNS[1])
    scores(1)
    sign_b(0)
    sign_a(0)
    sign_b(1)
    tt(diff(P1), z("a2m"), z("ta"), OP.subtract)
    tt(z("ad"), z("ta"), z("act"), OP.add)
    ts(value(U0), z("c48"), "p3", OP.add)
    ts(diff(U0), z("act"), 1.0, OP.add)
    wrap_a(0)
    cp(value(U1), value(P1))
    ts(value(U2), value(P1), 1.0, OP.add)

    def rest():
        ts(diff(U1), z("ta"), -1.0, OP.mult, -1.0, OP.add)
        ts(diff(U2), z("ad"), -1.0, OP.mult)
        cp(("mn", 192, C), ("mn", 0, 192))
        cp(("wl16", 0, 72), ("wlt", 0, 72))

    def rest2():
        ts(("inv", 0, 1), ("last", 0, 1), 1.0 - 1.0 / SMALL, OP.mult, 1.0 / SMALL, OP.add)
        ts(("inv3", 0, 1), ("last", 0, 1), (1.0 - 1.0 / SMALL) / 3.0, OP.mult, 1.0 / SMALL / 3.0, OP.add)

    for k in range(ROUNDS):
        new = "om1" if k % 2 == 0 else "om0"
        peer = T.cores[rank ^ STEP[k]]
        dl, la, last = "dl%d" % k, "la%d" % k, k == ROUNDS - 1
        sign_a(1)
        move("A", ("gr", 224, C), (("ew", 0, 2 * C), ("dst", 14, 24)))
        wrap_a(1)
        move("V", ("gr", 0, 224), (("ew", 0, 2 * C), ("dst", 0, 14)))
        tt(z("hw"), ends("aw"), z("ink"), OP.max)
        if k == 0: rest2()
        scan(("gs", 0, C), ("mk", 0, C), ("gr", 0, C), 0.0, OP.add)
        if k == 0:
            rest()
            halves(0)
        halves(1)

        def bit(i):
            tt(("ca", 48 * i, 48 * i + 48, 2), ends("gs"), z("hw"), OP.is_equal)

        def select(i, j):
            scan(("co", 48 * i, 48 * j), ("cb", 48 * i, 48 * j), ("ca", 48 * i, 48 * j), 0.0, OP.add)

        def cast(i, j):
            cp(("l16", 24 * i, 24 * j), ("co", 48 * i + 1, 48 * j, 2))
        for i in range(5): bit(i)
        select(P0, U0)
        select(U0, 5)
        cast(P0, U0)
        cast(U0, 5)

        def row(b, j, lo=0, hi=C):
            return (b, C * j + lo, C * j + hi) if k == 0 and b == "pir" else (b, 3 * lo + j, 3 * hi, 3)
        move("A", row("pir", 1), (("idr", 0, F), chosen(P1)))
        move("V", row("pir", 0), (("idr", 0, F), chosen(P0)))
        move("A", row("pir", 2, 0, 192), (("t2", 0, F), chosen(P1, 0, 192)))
        move("V", row("pir", 2, 192, C), (("t2", 0, F), chosen(P1, 192, C)))
        source = "pir"
        if k == 0:
            source = "om0"
            for q, j, lo, hi in (("V", 0, 0, C), ("A", 1, 0, C), ("V", 2, 0, 192), ("A", 2, 192, C)):
                move(q, row(source, j, lo, hi), (("pir", 0, F), ("wl16", 24 * j + lo // 16, 24 * j + hi // 16)))
        def rewire(q, j, lo=0, hi=C):
            move(q, row(new, j, lo, hi), ((source, 0, F), chosen((U0, U1, U2)[j], lo, hi)))

        def wrapped(j, lo=0, hi=C):
            wrap(("sc", C * j + lo, C * j + hi), row(new, j, lo, hi))

        def listed(j, lo=0, hi=C):
            agents(("l12", 24 * (j - 1) + lo // 16, 24 * (j - 1) + hi // 16), ("sc", C * j + lo + 15, C * j + hi, 16))
        cut = ZRUNS[0][1]
        rewire("V", 1, 0, cut)
        rewire("A", 2)
        rewire("V", 1, cut, C)
        rewire("A", 0)
        wrapped(1, 0, cut)
        wrapped(2)
        listed(1, 0, cut)
        wrapped(1, cut, C)
        listed(2)
        wrapped(0)
        listed(1, cut, C)
        ports((dl, 0, 24), ends("sc", 0))
        send(peer, T[la][:, 0:24], T[dl][:, 0:24], [(dl, 0, 24)], "al%d" % k)
        note("al%d" % k, len(topo.engines(core, peer)), [], [(la, 0, 24)])

        def level(i):
            if last: return
            if i == 0:
                ports(z("wi"), ends("sc", 0))
                tt(z("td"), W0, z("c3"), OP.subtract)
                tt(z("ad0"), W2, W1, OP.subtract)
            if i == 1: tt(z("act"), W0, z("wi"), OP.is_gt)
            if i == 2:
                tt(z("ta"), z("td"), z("act"), OP.mult)
                tt(z("ad"), z("ad0"), z("act"), OP.mult)
                flags()
            if i == 3:
                tt(value(P1), z("ta"), z("c31"), OP.add)
                tt(z("u10"), W1, z("ad"), OP.add)
                tt(("w", 0, 24), W2, z("ad"), OP.subtract)
                tt(diff(P1), z("a2m"), z("ta"), OP.subtract)
            if i == 4:
                ts(("x12", 0, 24), value(P1), 1.0, OP.add)
                cp(("x12", 24, 48), value(P1))
                tt(z("vta"), z("va"), value(P1), OP.add)
                tt(diff(U0), z("u10"), W0, OP.subtract)
        for i, (lo, hi) in enumerate(ZRUNS):
            for b in range(4): move("A", ("gz", C * b + lo, C * b + hi), (("xh", C * b, C * b + C), ("l12", lo // 16, hi // 16)))
        if not last:
            lin(("w", 24, 96), ends("sc", 0, 3), "inv", -1.0)
            lin(value(U0), ends("sc", 0), "inv", -1.0)

        def layer(i):
            lo, hi = ZRUNS[i]
            quant("zq", "zs", lo, hi, ("zt", 4 * lo, 4 * hi))
            for b in range(4): mm(4 * (i % 2) + b, hi - lo, "wq", "wp", 128 * b, "zq", "zs", lo)

        def evacuate(i):
            lo, hi = ZRUNS[i]
            for q, b in zip(EVACUATE[i], range(4)): scaled(q, ("hp", C * b + lo, C * b + hi), psum(4 * (i % 2) + b, hi - lo), 0.03125)
        for i, (lo, hi) in enumerate(ZRUNS):
            for b in range(4):
                tt(("zt", 4 * lo + b, 4 * hi, 4), (("xh", C * b, C * b + C), ("l12", 24 + lo // 16, 24 + hi // 16)), ("gz", C * b + lo, C * b + hi), OP.add)
                if i > 0 and b == 0: layer(i - 1)
        level(0)
        for i in range(len(ZRUNS) - 2): evacuate(i)
        layer(len(ZRUNS) - 1)
        move("A", ("mr", 0, C), ((new, 0, F), (la, 0, 24)))
        wrap(("ms", 0, C), ("mr", 0, C))
        level(1)
        evacuate(len(ZRUNS) - 2)
        agents(("ml", 0, 24), ends("ms"))
        level(2)
        evacuate(len(ZRUNS) - 1)
        hq, hs, lq, ls = "hq%d" % k, "hs%d" % k, "lq%d" % k, "ls%d" % k
        def pick(i, b):
            lo, hi = EXCHANGE[k][i]
            move(PICK[k][i][b], ("hg", 4 * lo + b, 4 * hi, 4), (("hp", C * b, C * b + C), ("ml", lo // 16, hi // 16)))
        for i, (lo, hi) in enumerate(EXCHANGE[k]):
            for b in range(4):
                if not (last and i > 0 and b == 3): pick(i, b)
            if i < 2: level(3 + i)
            if last and hi < C: pick(i + 1, 3)
            if last and hi == C: ports(("fin", 0, 72), ends("sc", 0, 3))
            quant(hq, hs, lo, hi, ("hg", 4 * lo, 4 * hi))
            send(peer, T[lq][:, lo:hi].bitcast(dt.uint8), T[hq][:, lo:hi].bitcast(dt.uint8), [(hq, lo, hi)], "ah%d%d" % (k, i))
            send(peer, T[ls][:, lo:hi], T[hs][:, lo:hi], [(hs, lo, hi)], "ah%d%d" % (k, i))
            note("ah%d%d" % (k, i), 2 * len(topo.engines(core, peer)), [], [(lq, lo, hi), (ls, lo, hi)])
        if k == 0:
            for j in range(3): iota(("qtab", j, F, 3), [[1, C]], C * j, 0, True)
        if not last:
            for j in range(2): move("A", ("y12", C * j, C * j + C), ((new, 0, F), ("x12", 24 * j, 24 * j + 24)))
            ts(z("dst"), z("vta"), 1.0 / 3.0, OP.mult)
            if k == 1: quant("vq", "vs", 0, 128, ("vt", 0, 512))
            wrap(("sy", 0, C), ("y12", 0, C))
        else:
            move("A", ("owr", 0, F), (("qtab", 0, F), ("fin", 0, 72)))
            for j in range(8): dma("S", T.ow[j:j + 1, :], T.owr[16 * j:16 * j + 1, 0:F], [("owr", 0, F)], [])
        def unpack(i):
            lo, hi = EXCHANGE[k][i]
            for b in range(4):
                e, es = ("em", "ems") if b // 2 == side else ("el", "els")
                mm(4 - 4 * (i % 2) + b, hi - lo, e, es, 128 * (b % 2), lq, ls, lo)

        def add(i):
            lo, hi = EXCHANGE[k][i]
            for b in range(4):
                x = ("xt", 4 * lo + b, 4 * hi, 4)
                tt(x, psum(4 - 4 * (i % 2) + b, hi - lo), x, OP.add)

        def store(bank, lo, hi):
            mm(bank, hi - lo, "vq", "vs", 0, "xq", "xs", lo)
            dma("S", T.oc[:, 4 * lo:4 * hi], T.xq[:, lo:hi].bitcast(dt.uint8), [("xq", lo, hi)], [])
            for j in range(4): dma("A" if j % 2 else "S", T.osc[4 * j:4 * j + 4, lo:hi], T.xs[32 * j:32 * j + 4, lo:hi], [("xs", lo, hi)], [])
            ac(("yt", lo, hi), psum(bank, hi - lo))
            dma("A", T.y[:, lo:hi], T.yt[:, lo:hi], [("yt", lo, hi)], [])
        n = len(EXCHANGE[k])
        state["runs"], state["bank"] = [(0, EXCHANGE[k][-1][0]), EXCHANGE[k][-1]], 4 - 4 * (n % 2)
        unpack(0)
        unpack(1)
        for i in range(n - 1):
            add(i)
            if i + 2 < n: unpack(i + 2)
        if not last:
            wrap(("sy", C, 2 * C), ("y12", C, 2 * C))
            lin(value(U2, 2), ends("sy", 0, 2), "inv", -1.0)
        quantx(*state["runs"][0])
        if not last:
            scores(0)
            halves(0)
            add(n - 1)
            tt(diff(U2, 2), ("w", 0, 48), value(U2, 2), OP.subtract)
            quantx(*state["runs"][1])
            scores(1)
            sign_b(0)
            sign_a(0)
            sign_b(1)
            wrap_a(0)
        else:
            store(state["bank"], *state["runs"][0])
            add(n - 1)
            quantx(*state["runs"][1])
            store(state["bank"] + 1, *state["runs"][1])
    for sem in ("V", "A", "P", "G", "left"): wait("G", sem, count[sem])
    for j in range(ndma[0]): wait("G", "d%d" % j, 16)
